import numpy as np
import ml_dtypes


def mxq(x, axis, fmt="e4m3"):
    dtype, down = {"e4m3": (ml_dtypes.float8_e4m3fn, 7), "e5m2": (ml_dtypes.float8_e5m2, 14)}[fmt]
    v = np.moveaxis(np.asarray(x, np.float32).astype(ml_dtypes.bfloat16).astype(np.float64), axis, -1)
    blocks = v.reshape(v.shape[:-1] + (-1, 32))
    amax = np.abs(blocks).max(-1, keepdims=True)
    byte = np.maximum(np.where(amax > 0, np.frexp(amax)[1] - 1 + 127, 0) - down, 1)
    scale = np.exp2(byte - 127.0)
    codes = (blocks / scale).astype(np.float32).astype(dtype).astype(np.float64)
    return np.moveaxis((codes * scale).reshape(v.shape), -1, axis)


WIDE = False


def mx_kscale(k):
    if not WIDE:
        return np.ones(k)
    levels = np.array([10, -10, 5, -5, 0])
    if k % 512:
        return np.exp2(np.random.permutation(np.resize(levels, k // 32))).repeat(32)
    a = np.empty((k // 512, 16))
    for p in range(k // 512):
        a[p, :8] = np.random.permutation(np.resize(levels, 8))
        for g in range(8):
            far = levels[np.abs(levels - a[p, g]) >= 10]
            a[p, g + 8] = far[np.random.randint(len(far))]
    return np.exp2(a.ravel()).repeat(32)


def f64(x):
    return np.asarray(x).astype(np.float64)


def striped(idx):
    return np.tile(idx.reshape(-1, 16).T, (8, 1)).astype(np.uint16)


def unstriped(offs):
    return offs[:16].T.reshape(-1).astype(np.int64)


E2M1 = np.array([0.0, 0.5, 1.0, 1.5, 2.0, 3.0, 4.0, 6.0, -0.0, -0.5, -1.0, -1.5, -2.0, -3.0, -4.0, -6.0])


def pack_weight(w, fmt):
    k, n = w.shape
    w = f64(np.asarray(w, np.float32).astype(ml_dtypes.bfloat16)).reshape(k // 32, 32, n)
    amax = np.abs(w).max(1)
    if fmt == "e4m3":
        byte = np.frexp(amax)[1] - 1 + 127 - 7
    else:
        mant, ex = np.frexp(amax / 6.0)
        byte = np.where(mant > 0.5, ex, ex - 1) + 127
    byte = np.clip(np.where(amax > 0, byte, 1), 1, 254)
    scaled = (w * np.exp2(127.0 - byte)[:, None, :]).reshape(k, n).astype(np.float32)
    by_word = np.ascontiguousarray(scaled.reshape(k // 512, 128, 4, n).transpose(0, 1, 3, 2))
    if fmt == "e4m3":
        words = by_word.astype(ml_dtypes.float8_e4m3fn).view(np.uint8)
    else:
        c = by_word.astype(ml_dtypes.float4_e2m1fn).view(np.uint8) & 0xF
        words = (c[..., 0::2] | (c[..., 1::2] << 4)).reshape(k // 512, 128, 2 * n)
    return np.ascontiguousarray(words), np.ascontiguousarray(byte.astype(np.uint8).reshape(k // 512, 16, n))


def unpack_weight(words, scales, fmt):
    g, _, n = scales.shape
    words = np.ascontiguousarray(words).reshape(g, 128, n, -1)
    if fmt == "e4m3":
        vals = words.view(ml_dtypes.float8_e4m3fn).astype(np.float64)
    else:
        nib = np.empty((g, 128, n, 4), np.uint8)
        nib[..., 0::2] = words & 0xF
        nib[..., 1::2] = words >> 4
        vals = E2M1[nib]
    vals = vals * np.repeat(np.exp2(scales.astype(np.float64) - 127.0), 8, axis=1)[..., None]
    return vals.transpose(0, 1, 3, 2).reshape(g * 512, n)


def silu(v):
    return v / (1.0 + np.exp(-np.maximum(v, -700.0)))


K, T, E, C, H, N = 512, 512, 4, 128, 1024, 128


def by_expert(wq, xq):
    return np.concatenate([wq[e].T @ xq[:, e * C:(e + 1) * C] for e in range(E)], axis=1)


def setup_inputs():
    n = np.random.standard_normal
    s = mx_kscale(K)[:, None]
    u = mx_kscale(H)
    x = pack_weight(n((K, T)) * s, "e4m3")
    return {
        "x_words": x[0],
        "x_scales": x[1],
        "w1": (n((E + 1, K, H)) / np.sqrt(K) / s[None]).astype(np.float32),
        "w3": (n((E + 1, K, H)) / np.sqrt(K) / s[None] * u[None, None, :]).astype(np.float32),
        "w2": (n((E + 1, H, N)) / np.sqrt(H) / u[None, :, None]).astype(np.float32),
        "gate": np.tile(np.random.uniform(0.2, 1.0, E * C), (N, 1)).astype(np.float32),
        "offs": striped(np.random.permutation(T)[:E * C]),
    }


def reference(x_words, x_scales, w1, w3, w2, gate, offs):
    idx = unstriped(offs)
    w1q, w3q, w2q = mxq(f64(w1), 1, "e4m3"), mxq(f64(w3), 1, "e4m3"), mxq(f64(w2), 1, "e4m3")
    xs = unpack_weight(x_words, x_scales, "e4m3")
    hs = silu(w1q[E].T @ xs) * (w3q[E].T @ xs)
    ys = w2q[E].T @ mxq(hs, 0, "e4m3")
    xq = unpack_weight(x_words, x_scales, "e4m3")[:, idx]
    h = silu(by_expert(w1q, xq))
    h = h * by_expert(w3q, xq)
    y = by_expert(w2q, mxq(h, 0, "e4m3"))
    out = ys
    out[:, idx] += f64(gate) * y
    return out

@@ -1,0 +1,189 @@
+from contextlib import ExitStack
+
+import concourse.mybir as mybir
+
+K, T, E, C, H, N = 512, 512, 4, 128, 1024, 128
+FLOPS = 2 * (E * C + T) * (2 * K * H + H * N)
+
+F32 = mybir.dt.float32
+BF16 = mybir.dt.bfloat16
+I32 = mybir.dt.int32
+U32 = mybir.dt.uint32
+U16 = mybir.dt.uint16
+U8 = mybir.dt.uint8
+FP8X4 = mybir.dt.float8_e4m3fn_x4
+MULT = mybir.AluOpType.mult
+ADD = mybir.AluOpType.add
+SILU = mybir.ActivationFunctionType.Silu
+
+P = 128
+PACK = 4
+KP = P * PACK
+PASSES = H // KP
+SHARED = E
+VEC_SHARED = 64
+VEC_ROUTED = 56
+VEC_LAST = 80
+VEC_SECOND = 0
+
+
+def tile_moe_shr_glu_silu_kernel(tc, x_words, x_scales, w1, w3, w2, gate, offs, out):
+    nc = tc.nc
+    with ExitStack() as ctx:
+        keep = ctx.enter_context(tc.tile_pool(name="keep", bufs=1))
+        rawp = ctx.enter_context(tc.tile_pool(name="rawp", bufs=8))
+        stage = ctx.enter_context(tc.tile_pool(name="stage", bufs=5))
+        wq = ctx.enter_context(tc.tile_pool(name="wq", bufs=8))
+        hp = ctx.enter_context(tc.tile_pool(name="hp", bufs=4))
+        pab = ctx.enter_context(tc.psum_pool(name="pab", bufs=3))
+        py = ctx.enter_context(tc.psum_pool(name="py", bufs=1))
+
+        offsets = keep.tile([P, E * C // 16], U16, name="offsets")
+        xw = keep.tile([P, T], I32, name="xw", align_bytes=64)
+        xs = keep.tile([P, T], U8, name="xs", align_bytes=64)
+        gw = keep.tile([P, E * C], U32, name="gw", align_bytes=64)
+        gs = keep.tile([P, E * C], U8, name="gs", align_bytes=64)
+        gate_sb = keep.tile([P, E * C], F32, name="gate_sb")
+        routed = keep.tile([P, T], F32, name="routed")
+        hs_codes = [keep.tile([P, T], U32, name="hs_codes%d" % g, align_bytes=64) for g in range(PASSES)]
+        hs_scales = [keep.tile([P, T], U8, name="hs_scales%d" % g, align_bytes=64) for g in range(PASSES)]
+        y_bank = py.tile([P, E * C], F32, name="y_bank")
+        ys_bank = py.tile([P, T], F32, name="ys_bank")
+
+        def load_first(w, e, c0, c1):
+            raw = rawp.tile([P, PACK, c1 - c0], F32, name="raw")
+            nc.sync.dma_start(out=raw[:], in_=w[e].rearrange("(p j) c -> p j c", j=PACK)[:, :, c0:c1])
+            return raw
+
+        def load_second(e):
+            raw = rawp.tile([P, PASSES, PACK * N], F32, name="raw")
+            nc.sync.dma_start(out=raw[:], in_=w2[e].rearrange("(g p j) n -> p g (j n)", p=P, j=PACK))
+            return raw
+
+        def quantize(grouped, width):
+            codes = wq.tile([P, width], U32, name="codes", align_bytes=64)
+            scales = wq.tile([P, width], U8, name="scales", align_bytes=64)
+            nc.vector.quantize_mx(out=codes[:].bitcast(FP8X4), scales=scales[:], in_=grouped[:])
+            return codes, scales
+
+        def share(dst, src, cut):
+            if cut > 0:
+                nc.vector.tensor_copy(out=dst[:, :cut], in_=src[:, :cut])
+            if cut < dst.shape[1]:
+                nc.scalar.copy(out=dst[:, cut:], in_=src[:, cut:])
+
+        def quantize_first(raw, c0, cut):
+            grouped = stage.tile([P, KP * PACK], BF16, name="grouped", align_bytes=64)
+            dst = grouped[:].rearrange("p (t m j) -> p m t j", t=PACK, j=PACK)
+            src = raw[:, :, c0:c0 + KP].rearrange("p j (m t) -> p m t j", t=PACK)
+            share(dst, src, cut)
+            return quantize(grouped, KP)
+
+        def quantize_second(raw, cut):
+            grouped = stage.tile([P, PASSES * N * PACK], BF16, name="grouped", align_bytes=64)
+            dst = grouped[:].rearrange("p (g c i j) -> p g c j i", g=PASSES, i=4, j=PACK)
+            src = raw[:].rearrange("p g (j c i) -> p g c j i", j=PACK, i=4)
+            share(dst, src, cut)
+            return quantize(grouped, PASSES * N)
+
+        def first_product(wcs, words, bytes_, tag):
+            bank = pab.tile([P, PACK, C], F32, name=tag)
+            for t in range(PACK):
+                cols = slice(t * P, (t + 1) * P)
+                nc.tensor.matmul_mx(out=bank[:, t, :], lhsT=wcs[0][:, cols].bitcast(FP8X4), lhsT_scale=wcs[1][:, cols],
+                                    rhs=words.bitcast(FP8X4), rhs_scale=bytes_, start=True, stop=True)
+            return bank
+
+        def activate(a_bank):
+            act = hp.tile([P, C, PACK], F32, name="act")
+            nc.scalar.activation(out=act[:], in_=a_bank[:].rearrange("p t c -> p c t"), func=SILU)
+            return act
+
+        def hidden(h, act, b_bank):
+            nc.vector.tensor_tensor(out=h.rearrange("p (c t) -> p c t", t=PACK), in0=b_bank[:].rearrange("p t c -> p c t"), in1=act[:], op=MULT)
+
+        def quantize_hidden(h, codes, scales):
+            nc.vector.quantize_mx(out=codes.bitcast(FP8X4), scales=scales, in_=h)
+
+        def second_product(q2, bank, h_ops):
+            for g in range(PASSES):
+                wc = slice(g * N, (g + 1) * N)
+                nc.tensor.matmul_mx(out=bank, lhsT=q2[0][:, wc].bitcast(FP8X4), lhsT_scale=q2[1][:, wc],
+                                    rhs=h_ops[g][0].bitcast(FP8X4), rhs_scale=h_ops[g][1], start=(g == 0), stop=(g == PASSES - 1))
+
+        nc.vector.memset(xs[:].bitcast(I32), 0)
+        nc.sync.dma_start(offsets[:], offs)
+        nc.sync.dma_start(out=xw[:], in_=x_words[0].rearrange("p t r -> p (t r)").bitcast(I32))
+        raw_1 = load_first(w1, SHARED, 0, KP)
+        for r in range(4):
+            nc.sync.dma_start(out=xs[:].bitcast(I32)[r:P:32, :], in_=x_scales[0].bitcast(I32)[r:16:4, :])
+        half = E * C // 2
+        for s in range(2):
+            lst = offsets[:, s * half // 16:(s + 1) * half // 16]
+            nc.vector.tensor_copy(gw[:, s * half:(s + 1) * half], xw[:].bitcast(U32).indirect(lst))
+        for s in range(2):
+            lst = offsets[:, s * half // 16:(s + 1) * half // 16]
+            nc.vector.tensor_copy(gs[:, s * half:(s + 1) * half], xs[:].indirect(lst))
+
+        for g in range(PASSES):
+            if g > 0:
+                raw_1 = load_first(w1, SHARED, g * KP, (g + 1) * KP)
+            raw_3 = load_first(w3, SHARED, g * KP, (g + 1) * KP)
+            q1 = quantize_first(raw_1, 0, VEC_SHARED)
+            q3 = quantize_first(raw_3, 0, VEC_SHARED)
+            hs = hp.tile([P, T * PACK], BF16, name="h", align_bytes=64)
+            for s in range(T // C):
+                cols = slice(s * C, (s + 1) * C)
+                act = activate(first_product(q1, xw[:, cols], xs[:, cols], "a_bank"))
+                b_bank = first_product(q3, xw[:, cols], xs[:, cols], "b_bank")
+                hidden(hs[:, s * KP:(s + 1) * KP], act, b_bank)
+            quantize_hidden(hs[:], hs_codes[g][:], hs_scales[g][:])
+        nc.sync.dma_start(out=gate_sb[:], in_=gate)
+
+        def second_layer(e, h_codes, h_scales, q2):
+            cols = slice(e * C, (e + 1) * C)
+            second_product(q2, y_bank[:, cols], [(h_codes[:, g * C:(g + 1) * C], h_scales[:, g * C:(g + 1) * C]) for g in range(PASSES)])
+            y_sb = hp.tile([P, C], F32, name="y_sb")
+            nc.scalar.copy(out=y_sb[:], in_=y_bank[:, cols])
+            nc.vector.tensor_tensor(routed[:].indirect(offsets[:, e * C // 16:(e + 1) * C // 16]), y_sb[:], gate_sb[:, cols], MULT)
+
+        pending = None
+        for e in range(E):
+            cols = slice(e * C, (e + 1) * C)
+            last = e == E - 1
+            whole = True and not last
+            h = hp.tile([P, PASSES * KP], BF16, name="h", align_bytes=64)
+            h_codes = hp.tile([P, PASSES * C], U32, name="h_codes", align_bytes=64)
+            h_scales = hp.tile([P, PASSES * C], U8, name="h_scales", align_bytes=64)
+            if whole:
+                raw_1 = load_first(w1, e, 0, H)
+                acts = [activate(first_product(quantize_first(raw_1, g * KP, VEC_ROUTED), gw[:, cols], gs[:, cols], "a_bank")) for g in range(PASSES)]
+                if pending is not None:
+                    second_layer(*pending, quantize_second(load_second(e - 1), VEC_SECOND))
+                raw_3 = load_first(w3, e, 0, H)
+                for g in range(PASSES):
+                    q3 = quantize_first(raw_3, g * KP, VEC_ROUTED)
+                    hidden(h[:, g * KP:(g + 1) * KP], acts[g], first_product(q3, gw[:, cols], gs[:, cols], "b_bank"))
+                quantize_hidden(h[:], h_codes[:], h_scales[:])
+            else:
+                for g in range(PASSES):
+                    q1 = quantize_first(load_first(w1, e, g * KP, (g + 1) * KP), 0, VEC_ROUTED)
+                    act = activate(first_product(q1, gw[:, cols], gs[:, cols], "a_bank"))
+                    if g == 0 and pending is not None and not (last and True):
+                        second_layer(*pending, quantize_second(load_second(e - 1), VEC_SECOND))
+                    q3 = quantize_first(load_first(w3, e, g * KP, (g + 1) * KP), 0, VEC_LAST if last and g == 1 else VEC_ROUTED)
+                    hidden(h[:, g * KP:(g + 1) * KP], act, first_product(q3, gw[:, cols], gs[:, cols], "b_bank"))
+                    if last:
+                        quantize_hidden(h[:, g * KP:(g + 1) * KP], h_codes[:, g * C:(g + 1) * C], h_scales[:, g * C:(g + 1) * C])
+                if not last:
+                    quantize_hidden(h[:], h_codes[:], h_scales[:])
+            if last and True:
+                second_layer(*pending, quantize_second(load_second(e - 1), VEC_SECOND))
+            pending = (e, h_codes, h_scales)
+        second_layer(*pending, quantize_second(load_second(E - 1), 0))
+        second_product(quantize_second(load_second(SHARED), 0), ys_bank[:], [(hs_codes[g][:], hs_scales[g][:]) for g in range(PASSES)])
+        for s in range(2):
+            cols = slice(s * T // 2, (s + 1) * T // 2)
+            res = hp.tile([P, T // 2], F32, name="res")
+            nc.vector.tensor_tensor(out=res[:], in0=ys_bank[:, cols], in1=routed[:, cols], op=ADD)
+            nc.sync.dma_start(out=out[:, cols], in_=res[:])

@@ -74,9 +74,12 @@ def tile_moe_shr_glu_silu_kernel(tc, x_words, x_scales, w1, w3, w2, gate, offs, 
 
         def quantize_first(raw, c0, cut):
             grouped = stage.tile([P, KP * PACK], BF16, name="grouped", align_bytes=64)
-            dst = grouped[:].rearrange("p (t m j) -> p m t j", t=PACK, j=PACK)
-            src = raw[:, :, c0:c0 + KP].rearrange("p j (m t) -> p m t j", t=PACK)
-            share(dst, src, cut)
+            dst = grouped[:].rearrange("p (u v m j) -> p u m j v", u=2, v=2, j=PACK)
+            src = raw[:, :, c0:c0 + KP].rearrange("p j (m u v) -> p u m j v", u=2, v=2)
+            if cut > 0:
+                nc.vector.tensor_copy(out=dst[:, :, :cut], in_=src[:, :, :cut])
+            if cut < P:
+                nc.scalar.copy(out=dst[:, :, cut:], in_=src[:, :, cut:])
             return quantize(grouped, KP)
 
         def quantize_second(raw, cut):
@@ -95,12 +98,12 @@ def tile_moe_shr_glu_silu_kernel(tc, x_words, x_scales, w1, w3, w2, gate, offs, 
             return bank
 
         def activate(a_bank):
-            act = hp.tile([P, C, PACK], F32, name="act")
-            nc.scalar.activation(out=act[:], in_=a_bank[:].rearrange("p t c -> p c t"), func=SILU)
+            act = hp.tile([P, C // 2, PACK, 2], F32, name="act")
+            nc.scalar.activation(out=act[:], in_=a_bank[:].rearrange("p t (c d) -> p c t d", d=2), func=SILU)
             return act
 
         def hidden(h, act, b_bank):
-            nc.vector.tensor_tensor(out=h.rearrange("p (c t) -> p c t", t=PACK), in0=b_bank[:].rearrange("p t c -> p c t"), in1=act[:], op=MULT)
+            nc.vector.tensor_tensor(out=h.rearrange("p (c d t) -> p c t d", d=2, t=PACK), in0=b_bank[:].rearrange("p t (c d) -> p c t d", d=2), in1=act[:], op=MULT)
 
         def quantize_hidden(h, codes, scales):
             nc.vector.quantize_mx(out=codes.bitcast(FP8X4), scales=scales, in_=h)

@@ -21,21 +21,20 @@ PACK = 4
 KP = P * PACK
 PASSES = H // KP
 SHARED = E
-VEC_SHARED = 64
-VEC_ROUTED = 56
-VEC_LAST = 80
-VEC_SECOND = 0
+RING = 6
+HRING = 4
 
 
 def tile_moe_shr_glu_silu_kernel(tc, x_words, x_scales, w1, w3, w2, gate, offs, out):
     nc = tc.nc
     with ExitStack() as ctx:
         keep = ctx.enter_context(tc.tile_pool(name="keep", bufs=1))
-        rawp = ctx.enter_context(tc.tile_pool(name="rawp", bufs=8))
-        stage = ctx.enter_context(tc.tile_pool(name="stage", bufs=5))
-        wq = ctx.enter_context(tc.tile_pool(name="wq", bufs=8))
-        hp = ctx.enter_context(tc.tile_pool(name="hp", bufs=4))
-        pab = ctx.enter_context(tc.psum_pool(name="pab", bufs=3))
+        ring = ctx.enter_context(tc.tile_pool(name="ring", bufs=1))
+        stage = ctx.enter_context(tc.tile_pool(name="stage", bufs=3))
+        wq = ctx.enter_context(tc.tile_pool(name="wq", bufs=4))
+        hp = ctx.enter_context(tc.tile_pool(name="hp", bufs=3))
+        pa = ctx.enter_context(tc.psum_pool(name="pa", bufs=2))
+        pb = ctx.enter_context(tc.psum_pool(name="pb", bufs=4))
         py = ctx.enter_context(tc.psum_pool(name="py", bufs=1))
 
         offsets = keep.tile([P, E * C // 16], U16, name="offsets")
@@ -45,148 +44,155 @@ def tile_moe_shr_glu_silu_kernel(tc, x_words, x_scales, w1, w3, w2, gate, offs, 
         gs = keep.tile([P, E * C], U8, name="gs", align_bytes=64)
         gate_sb = keep.tile([P, E * C], F32, name="gate_sb")
         routed = keep.tile([P, T], F32, name="routed")
-        hs_codes = [keep.tile([P, T], U32, name="hs_codes%d" % g, align_bytes=64) for g in range(PASSES)]
-        hs_scales = [keep.tile([P, T], U8, name="hs_scales%d" % g, align_bytes=64) for g in range(PASSES)]
         y_bank = py.tile([P, E * C], F32, name="y_bank")
         ys_bank = py.tile([P, T], F32, name="ys_bank")
 
-        def load_first(w, e, c0, c1):
-            raw = rawp.tile([P, PACK, c1 - c0], F32, name="raw")
-            nc.sync.dma_start(out=raw[:], in_=w[e].rearrange("(p j) c -> p j c", j=PACK)[:, :, c0:c1])
+        steps = [(e, g) for e in [SHARED] + list(range(E)) for g in range(PASSES)]
+        last = len(steps) - 1
+
+        def groups(s):
+            e = steps[s][0]
+            if e == SHARED:
+                return [(xw[:, i * C:(i + 1) * C], xs[:, i * C:(i + 1) * C]) for i in range(T // C)]
+            return [(gw[:, e * C:(e + 1) * C], gs[:, e * C:(e + 1) * C])]
+
+        def load_first(w, s, raw):
+            e, g = steps[s]
+            nc.sync.dma_start(out=raw[:], in_=w[e].rearrange("(p j) c -> p j c", j=PACK)[:, :, g * KP:(g + 1) * KP])
             return raw
 
         def load_second(e):
-            raw = rawp.tile([P, PASSES, PACK * N], F32, name="raw")
+            raw = keep.tile([P, PASSES, PACK * N], F32, name="raw2_%d" % e)
             nc.sync.dma_start(out=raw[:], in_=w2[e].rearrange("(g p j) n -> p g (j n)", p=P, j=PACK))
             return raw
 
-        def quantize(grouped, width):
-            codes = wq.tile([P, width], U32, name="codes", align_bytes=64)
-            scales = wq.tile([P, width], U8, name="scales", align_bytes=64)
+        def quantize(grouped, codes):
+            scales = wq.tile([P, codes.shape[1]], U8, name="scales", align_bytes=64, bufs=8)
             nc.vector.quantize_mx(out=codes[:].bitcast(FP8X4), scales=scales[:], in_=grouped[:])
             return codes, scales
 
-        def share(dst, src, cut):
+        def round_first(raw, grouped, cut):
+            dst = grouped[:].rearrange("p (u v m j) -> p u m j v", u=2, v=2, j=PACK)
+            src = raw[:].rearrange("p j (m u v) -> p u m j v", u=2, v=2)
             if cut > 0:
                 nc.vector.tensor_copy(out=dst[:, :cut], in_=src[:, :cut])
-            if cut < dst.shape[1]:
+            if cut < 2:
                 nc.scalar.copy(out=dst[:, cut:], in_=src[:, cut:])
+            return grouped
 
-        def quantize_first(raw, c0, cut):
-            grouped = stage.tile([P, KP * PACK], BF16, name="grouped", align_bytes=64)
-            dst = grouped[:].rearrange("p (u v m j) -> p u m j v", u=2, v=2, j=PACK)
-            src = raw[:, :, c0:c0 + KP].rearrange("p j (m u v) -> p u m j v", u=2, v=2)
-            if cut > 0:
-                nc.vector.tensor_copy(out=dst[:, :, :cut], in_=src[:, :, :cut])
-            if cut < P:
-                nc.scalar.copy(out=dst[:, :, cut:], in_=src[:, :, cut:])
-            return quantize(grouped, KP)
-
-        def quantize_second(raw, cut):
-            grouped = stage.tile([P, PASSES * N * PACK], BF16, name="grouped", align_bytes=64)
+        def quantize_second(raw):
+            grouped = stage.tile([P, PASSES * N * PACK], BF16, name="grouped2", align_bytes=64)
             dst = grouped[:].rearrange("p (g c i j) -> p g c j i", g=PASSES, i=4, j=PACK)
             src = raw[:].rearrange("p g (j c i) -> p g c j i", j=PACK, i=4)
-            share(dst, src, cut)
-            return quantize(grouped, PASSES * N)
+            nc.scalar.copy(out=dst, in_=src)
+            return quantize(grouped, wq.tile([P, PASSES * N], U32, name="codes2", align_bytes=64))
 
-        def first_product(wcs, words, bytes_, tag):
-            bank = pab.tile([P, PACK, C], F32, name=tag)
+        def first_product(wcs, tokens, bank):
             for t in range(PACK):
                 cols = slice(t * P, (t + 1) * P)
                 nc.tensor.matmul_mx(out=bank[:, t, :], lhsT=wcs[0][:, cols].bitcast(FP8X4), lhsT_scale=wcs[1][:, cols],
-                                    rhs=words.bitcast(FP8X4), rhs_scale=bytes_, start=True, stop=True)
+                                    rhs=tokens[0].bitcast(FP8X4), rhs_scale=tokens[1], start=True, stop=True)
             return bank
 
-        def activate(a_bank):
-            act = hp.tile([P, C // 2, PACK, 2], F32, name="act")
-            nc.scalar.activation(out=act[:], in_=a_bank[:].rearrange("p t (c d) -> p c t d", d=2), func=SILU)
-            return act
+        def activate(q1, s):
+            acts = []
+            act_all = ring.tile([P, len(groups(s)), KP], F32, name="raw3_%d" % (s % RING))
+            for i, tokens in enumerate(groups(s)):
+                a_bank = first_product(q1, tokens, pa.tile([P, PACK, C], F32, name="a_bank"))
+                act = act_all[:, i, :].rearrange("p (c t d) -> p c t d", t=PACK, d=2)
+                nc.scalar.activation(out=act, in_=a_bank[:].rearrange("p t (c d) -> p c t d", d=2), func=SILU, bias=zero[:])
+                acts.append(act)
+            return acts
 
-        def hidden(h, act, b_bank):
-            nc.vector.tensor_tensor(out=h.rearrange("p (c d t) -> p c t d", d=2, t=PACK), in0=b_bank[:].rearrange("p t (c d) -> p c t d", d=2), in1=act[:], op=MULT)
+        def gate_products(q3, s):
+            return [first_product(q3, tokens, pb.tile([P, PACK, C], F32, name="b_bank")) for tokens in groups(s)]
 
-        def quantize_hidden(h, codes, scales):
-            nc.vector.quantize_mx(out=codes.bitcast(FP8X4), scales=scales, in_=h)
+        def hidden(q3, acts, s):
+            h = hp.tile([P, len(acts) * KP], BF16, name="h", align_bytes=64)
+            for i, tokens in enumerate(groups(s)):
+                b_bank = first_product(q3, tokens, pb.tile([P, PACK, C], F32, name="b_bank"))
+                nc.vector.tensor_tensor(out=h[:, i * KP:(i + 1) * KP].rearrange("p (c d t) -> p c t d", d=2, t=PACK),
+                                        in0=b_bank[:].rearrange("p t (c d) -> p c t d", d=2), in1=acts[i], op=MULT)
+            return h
 
-        def second_product(q2, bank, h_ops):
+        def quantize_hidden(h, s, codes):
+            scales = keep.tile([P, codes.shape[1]], U8, name="h_scales%d" % s, align_bytes=64)
+            nc.vector.quantize_mx(out=codes[:].bitcast(FP8X4), scales=scales[:], in_=h[:])
+            return codes, scales
+
+        def second_product(e, bank):
+            q2 = w2q[e]
             for g in range(PASSES):
                 wc = slice(g * N, (g + 1) * N)
+                hq = hqs[steps.index((e, g))]
                 nc.tensor.matmul_mx(out=bank, lhsT=q2[0][:, wc].bitcast(FP8X4), lhsT_scale=q2[1][:, wc],
-                                    rhs=h_ops[g][0].bitcast(FP8X4), rhs_scale=h_ops[g][1], start=(g == 0), stop=(g == PASSES - 1))
+                                    rhs=hq[0][:].bitcast(FP8X4), rhs_scale=hq[1][:], start=(g == 0), stop=(g == PASSES - 1))
 
-        nc.vector.memset(xs[:].bitcast(I32), 0)
-        nc.sync.dma_start(offsets[:], offs)
-        nc.sync.dma_start(out=xw[:], in_=x_words[0].rearrange("p t r -> p (t r)").bitcast(I32))
-        raw_1 = load_first(w1, SHARED, 0, KP)
-        for r in range(4):
-            nc.sync.dma_start(out=xs[:].bitcast(I32)[r:P:32, :], in_=x_scales[0].bitcast(I32)[r:16:4, :])
-        half = E * C // 2
-        for s in range(2):
-            lst = offsets[:, s * half // 16:(s + 1) * half // 16]
-            nc.vector.tensor_copy(gw[:, s * half:(s + 1) * half], xw[:].bitcast(U32).indirect(lst))
-        for s in range(2):
-            lst = offsets[:, s * half // 16:(s + 1) * half // 16]
-            nc.vector.tensor_copy(gs[:, s * half:(s + 1) * half], xs[:].indirect(lst))
-
-        for g in range(PASSES):
-            if g > 0:
-                raw_1 = load_first(w1, SHARED, g * KP, (g + 1) * KP)
-            raw_3 = load_first(w3, SHARED, g * KP, (g + 1) * KP)
-            q1 = quantize_first(raw_1, 0, VEC_SHARED)
-            q3 = quantize_first(raw_3, 0, VEC_SHARED)
-            hs = hp.tile([P, T * PACK], BF16, name="h", align_bytes=64)
-            for s in range(T // C):
-                cols = slice(s * C, (s + 1) * C)
-                act = activate(first_product(q1, xw[:, cols], xs[:, cols], "a_bank"))
-                b_bank = first_product(q3, xw[:, cols], xs[:, cols], "b_bank")
-                hidden(hs[:, s * KP:(s + 1) * KP], act, b_bank)
-            quantize_hidden(hs[:], hs_codes[g][:], hs_scales[g][:])
-        nc.sync.dma_start(out=gate_sb[:], in_=gate)
-
-        def second_layer(e, h_codes, h_scales, q2):
+        def send_back(e):
             cols = slice(e * C, (e + 1) * C)
-            second_product(q2, y_bank[:, cols], [(h_codes[:, g * C:(g + 1) * C], h_scales[:, g * C:(g + 1) * C]) for g in range(PASSES)])
+            second_product(e, y_bank[:, cols])
             y_sb = hp.tile([P, C], F32, name="y_sb")
             nc.scalar.copy(out=y_sb[:], in_=y_bank[:, cols])
             nc.vector.tensor_tensor(routed[:].indirect(offsets[:, e * C // 16:(e + 1) * C // 16]), y_sb[:], gate_sb[:, cols], MULT)
 
-        pending = None
-        for e in range(E):
-            cols = slice(e * C, (e + 1) * C)
-            last = e == E - 1
-            whole = True and not last
-            h = hp.tile([P, PASSES * KP], BF16, name="h", align_bytes=64)
-            h_codes = hp.tile([P, PASSES * C], U32, name="h_codes", align_bytes=64)
-            h_scales = hp.tile([P, PASSES * C], U8, name="h_scales", align_bytes=64)
-            if whole:
-                raw_1 = load_first(w1, e, 0, H)
-                acts = [activate(first_product(quantize_first(raw_1, g * KP, VEC_ROUTED), gw[:, cols], gs[:, cols], "a_bank")) for g in range(PASSES)]
-                if pending is not None:
-                    second_layer(*pending, quantize_second(load_second(e - 1), VEC_SECOND))
-                raw_3 = load_first(w3, e, 0, H)
-                for g in range(PASSES):
-                    q3 = quantize_first(raw_3, g * KP, VEC_ROUTED)
-                    hidden(h[:, g * KP:(g + 1) * KP], acts[g], first_product(q3, gw[:, cols], gs[:, cols], "b_bank"))
-                quantize_hidden(h[:], h_codes[:], h_scales[:])
-            else:
-                for g in range(PASSES):
-                    q1 = quantize_first(load_first(w1, e, g * KP, (g + 1) * KP), 0, VEC_ROUTED)
-                    act = activate(first_product(q1, gw[:, cols], gs[:, cols], "a_bank"))
-                    if g == 0 and pending is not None and not (last and True):
-                        second_layer(*pending, quantize_second(load_second(e - 1), VEC_SECOND))
-                    q3 = quantize_first(load_first(w3, e, g * KP, (g + 1) * KP), 0, VEC_LAST if last and g == 1 else VEC_ROUTED)
-                    hidden(h[:, g * KP:(g + 1) * KP], act, first_product(q3, gw[:, cols], gs[:, cols], "b_bank"))
-                    if last:
-                        quantize_hidden(h[:, g * KP:(g + 1) * KP], h_codes[:, g * C:(g + 1) * C], h_scales[:, g * C:(g + 1) * C])
-                if not last:
-                    quantize_hidden(h[:], h_codes[:], h_scales[:])
-            if last and True:
-                second_layer(*pending, quantize_second(load_second(e - 1), VEC_SECOND))
-            pending = (e, h_codes, h_scales)
-        second_layer(*pending, quantize_second(load_second(E - 1), 0))
-        second_product(quantize_second(load_second(SHARED), 0), ys_bank[:], [(hs_codes[g][:], hs_scales[g][:]) for g in range(PASSES)])
-        for s in range(2):
-            cols = slice(s * T // 2, (s + 1) * T // 2)
+        def raw1_tile(s):
+            return ring.tile([P, PACK, KP], F32, name="raw1_%d" % (s % RING), align_bytes=64)
+
+        nc.vector.memset(xs[:].bitcast(I32), 0)
+        zero_in = keep.tile([P, 1], F32, name="zero_in")
+        zero = keep.tile([P, 1], F32, name="zero")
+        nc.vector.memset(zero_in[:], 0.0)
+        nc.scalar.activation(out=zero[:], in_=zero_in[:], func=SILU)
+        nc.sync.dma_start(offsets[:], offs)
+        nc.sync.dma_start(out=xw[:], in_=x_words[0].rearrange("p t r -> p (t r)").bitcast(I32))
+        for r in range(4):
+            nc.sync.dma_start(out=xs[:].bitcast(I32)[r:P:32, :], in_=x_scales[0].bitcast(I32)[r:16:4, :])
+        raw1 = load_first(w1, 0, raw1_tile(0))
+        half = E * C // 2
+        for i in range(2):
+            nc.vector.tensor_copy(gw[:, i * half:(i + 1) * half], xw[:].bitcast(U32).indirect(offsets[:, i * half // 16:(i + 1) * half // 16]))
+        for i in range(2):
+            nc.vector.tensor_copy(gs[:, i * half:(i + 1) * half], xs[:].indirect(offsets[:, i * half // 16:(i + 1) * half // 16]))
+
+        w2q, hqs, hs, acts, grouped3, raw2 = {}, {}, {}, {}, {}, {}
+        for s in range(last + 1):
+            e, g = steps[s]
+            if s > 0:
+                raw1 = load_first(w1, s, raw1_tile(s))
+            due = (s - 4) // 2 if s % 2 == 0 else -1
+            raw3 = load_first(w3, s, ring.tile([P, PACK, KP], F32, name="raw3_%d" % (s % RING)))
+            if due in range(E - 2):
+                raw2[due] = load_second(due)
+            if s == 2:
+                nc.sync.dma_start(out=gate_sb[:], in_=gate)
+            grouped1 = round_first(raw1, stage.tile([P, KP * PACK], BF16, name="grouped1", align_bytes=64), 2)
+            if s >= 1:
+                q3 = quantize(grouped3[s - 1], wq.tile([P, KP], U32, name="codes3", align_bytes=64))
+            if s >= 2:
+                hqs[s - 2] = quantize_hidden(hs[s - 2], s - 2, keep.tile([P, len(groups(s - 2)) * C], U32, name="h_codes%d" % s, align_bytes=64))
+            q1 = quantize(grouped1, wq.tile([P, KP], U32, name="codes1", align_bytes=64))
+            grouped3[s] = round_first(raw3, ring.tile([P, KP * PACK], BF16, name="grouped3_%d" % (s % HRING), align_bytes=64), 1 if s == last else 0)
+            if s >= 1:
+                hs[s - 1] = hidden(q3, acts[s - 1], s - 1)
+            acts[s] = activate(q1, s)
+            if due in raw2:
+                w2q[due] = quantize_second(raw2[due])
+            back = (s - 5) // 2 if s % 2 == 1 else -1
+            if back in w2q:
+                send_back(back)
+        for e in list(range(E - 2, E)) + [SHARED]:
+            raw2[e] = load_second(e)
+        q3 = quantize(grouped3[last], wq.tile([P, KP], U32, name="codes3", align_bytes=64))
+        hqs[last - 1] = quantize_hidden(hs[last - 1], last - 1, keep.tile([P, C], U32, name="h_codes_a", align_bytes=64))
+        hs[last] = hidden(q3, acts[last], last)
+        hqs[last] = quantize_hidden(hs[last], last, keep.tile([P, C], U32, name="h_codes_b", align_bytes=64))
+        for e in range(E - 2, E):
+            w2q[e] = quantize_second(raw2[e])
+            send_back(e)
+        w2q[SHARED] = quantize_second(raw2[SHARED])
+        second_product(SHARED, ys_bank[:])
+        for i in range(2):
+            cols = slice(i * T // 2, (i + 1) * T // 2)
             res = hp.tile([P, T // 2], F32, name="res")
             nc.vector.tensor_tensor(out=res[:], in0=ys_bank[:, cols], in1=routed[:, cols], op=ADD)
             nc.sync.dma_start(out=out[:, cols], in_=res[:])

@@ -21,7 +21,7 @@ PACK = 4
 KP = P * PACK
 PASSES = H // KP
 SHARED = E
-RING = 6
+RING = 4
 HRING = 4
 
 
@@ -33,8 +33,8 @@ def tile_moe_shr_glu_silu_kernel(tc, x_words, x_scales, w1, w3, w2, gate, offs, 
         stage = ctx.enter_context(tc.tile_pool(name="stage", bufs=3))
         wq = ctx.enter_context(tc.tile_pool(name="wq", bufs=4))
         hp = ctx.enter_context(tc.tile_pool(name="hp", bufs=3))
-        pa = ctx.enter_context(tc.psum_pool(name="pa", bufs=2))
-        pb = ctx.enter_context(tc.psum_pool(name="pb", bufs=4))
+        pa = ctx.enter_context(tc.psum_pool(name="pa", bufs=4))
+        pb = ctx.enter_context(tc.psum_pool(name="pb", bufs=2))
         py = ctx.enter_context(tc.psum_pool(name="py", bufs=1))
 
         offsets = keep.tile([P, E * C // 16], U16, name="offsets")
@@ -56,13 +56,13 @@ def tile_moe_shr_glu_silu_kernel(tc, x_words, x_scales, w1, w3, w2, gate, offs, 
                 return [(xw[:, i * C:(i + 1) * C], xs[:, i * C:(i + 1) * C]) for i in range(T // C)]
             return [(gw[:, e * C:(e + 1) * C], gs[:, e * C:(e + 1) * C])]
 
-        def load_first(w, s, raw):
-            e, g = steps[s]
-            nc.sync.dma_start(out=raw[:], in_=w[e].rearrange("(p j) c -> p j c", j=PACK)[:, :, g * KP:(g + 1) * KP])
+        def load_first(w, e, passes, name):
+            raw = ring.tile([P, PACK, len(passes) * KP], F32, name=name)
+            nc.sync.dma_start(out=raw[:], in_=w[e].rearrange("(p j) c -> p j c", j=PACK)[:, :, passes[0] * KP:(passes[-1] + 1) * KP])
             return raw
 
-        def load_second(e):
-            raw = keep.tile([P, PASSES, PACK * N], F32, name="raw2_%d" % e)
+        def load_second(e, name):
+            raw = ring.tile([P, PASSES, PACK * N], F32, name=name)
             nc.sync.dma_start(out=raw[:], in_=w2[e].rearrange("(g p j) n -> p g (j n)", p=P, j=PACK))
             return raw
 
@@ -73,7 +73,7 @@ def tile_moe_shr_glu_silu_kernel(tc, x_words, x_scales, w1, w3, w2, gate, offs, 
 
         def round_first(raw, grouped, cut):
             dst = grouped[:].rearrange("p (u v m j) -> p u m j v", u=2, v=2, j=PACK)
-            src = raw[:].rearrange("p j (m u v) -> p u m j v", u=2, v=2)
+            src = raw.rearrange("p j (m u v) -> p u m j v", u=2, v=2)
             if cut > 0:
                 nc.vector.tensor_copy(out=dst[:, :cut], in_=src[:, :cut])
             if cut < 2:
@@ -94,18 +94,17 @@ def tile_moe_shr_glu_silu_kernel(tc, x_words, x_scales, w1, w3, w2, gate, offs, 
                                     rhs=tokens[0].bitcast(FP8X4), rhs_scale=tokens[1], start=True, stop=True)
             return bank
 
-        def activate(q1, s):
-            acts = []
-            act_all = ring.tile([P, len(groups(s)), KP], F32, name="raw3_%d" % (s % RING))
-            for i, tokens in enumerate(groups(s)):
-                a_bank = first_product(q1, tokens, pa.tile([P, PACK, C], F32, name="a_bank"))
-                act = act_all[:, i, :].rearrange("p (c t d) -> p c t d", t=PACK, d=2)
-                nc.scalar.activation(out=act, in_=a_bank[:].rearrange("p t (c d) -> p c t d", d=2), func=SILU, bias=zero[:])
-                acts.append(act)
-            return acts
-
-        def gate_products(q3, s):
-            return [first_product(q3, tokens, pb.tile([P, PACK, C], F32, name="b_bank")) for tokens in groups(s)]
+        def activate(q1s, ss, name):
+            act_all = ring.tile([P, sum(len(groups(s)) for s in ss), KP], F32, name=name)
+            i = 0
+            for q1, s in zip(q1s, ss):
+                acts[s] = []
+                for tokens in groups(s):
+                    a_bank = first_product(q1, tokens, pa.tile([P, PACK, C], F32, name="a_bank"))
+                    act = act_all[:, i, :].rearrange("p (c t d) -> p c t d", t=PACK, d=2)
+                    nc.scalar.activation(out=act, in_=a_bank[:].rearrange("p t (c d) -> p c t d", d=2), func=SILU, bias=zero[:])
+                    acts[s].append(act)
+                    i = i + 1
 
         def hidden(q3, acts, s):
             h = hp.tile([P, len(acts) * KP], BF16, name="h", align_bytes=64)
@@ -135,9 +134,6 @@ def tile_moe_shr_glu_silu_kernel(tc, x_words, x_scales, w1, w3, w2, gate, offs, 
             nc.scalar.copy(out=y_sb[:], in_=y_bank[:, cols])
             nc.vector.tensor_tensor(routed[:].indirect(offsets[:, e * C // 16:(e + 1) * C // 16]), y_sb[:], gate_sb[:, cols], MULT)
 
-        def raw1_tile(s):
-            return ring.tile([P, PACK, KP], F32, name="raw1_%d" % (s % RING), align_bytes=64)
-
         nc.vector.memset(xs[:].bitcast(I32), 0)
         zero_in = keep.tile([P, 1], F32, name="zero_in")
         zero = keep.tile([P, 1], F32, name="zero")
@@ -147,49 +143,57 @@ def tile_moe_shr_glu_silu_kernel(tc, x_words, x_scales, w1, w3, w2, gate, offs, 
         nc.sync.dma_start(out=xw[:], in_=x_words[0].rearrange("p t r -> p (t r)").bitcast(I32))
         for r in range(4):
             nc.sync.dma_start(out=xs[:].bitcast(I32)[r:P:32, :], in_=x_scales[0].bitcast(I32)[r:16:4, :])
-        raw1 = load_first(w1, 0, raw1_tile(0))
         half = E * C // 2
         for i in range(2):
             nc.vector.tensor_copy(gw[:, i * half:(i + 1) * half], xw[:].bitcast(U32).indirect(offsets[:, i * half // 16:(i + 1) * half // 16]))
         for i in range(2):
             nc.vector.tensor_copy(gs[:, i * half:(i + 1) * half], xs[:].indirect(offsets[:, i * half // 16:(i + 1) * half // 16]))
 
-        w2q, hqs, hs, acts, grouped3, raw2 = {}, {}, {}, {}, {}, {}
-        for s in range(last + 1):
-            e, g = steps[s]
-            if s > 0:
-                raw1 = load_first(w1, s, raw1_tile(s))
-            due = (s - 4) // 2 if s % 2 == 0 else -1
-            raw3 = load_first(w3, s, ring.tile([P, PACK, KP], F32, name="raw3_%d" % (s % RING)))
-            if due in range(E - 2):
-                raw2[due] = load_second(due)
-            if s == 2:
+        w2q, hqs, acts = {}, {}, {}
+        blocks = [(SHARED, [0, 1])] + [(e, [0, 1]) for e in range(E)]
+        n1 = 0
+        n3 = 0
+        for b, (e, passes) in enumerate(blocks):
+            final = b == len(blocks) - 1
+            ss = [steps.index((e, g)) for g in passes]
+            raw1 = load_first(w1, e, passes, "raw1_%d" % (n1 % RING))
+            n1 = n1 + 1
+            if final and True:
+                raw2 = load_second(e - 1, "raw1_%d" % (n1 % RING))
+                n1 = n1 + 1
+            raw3s = []
+            for part in ([[g] for g in passes] if final else [passes]):
+                name3 = "raw3_%d" % (n3 % RING)
+                raw = load_first(w3, e, part, name3)
+                raw3s.extend([raw[:, :, i * KP:(i + 1) * KP] for i in range(len(part))])
+                n3 = n3 + 1
+            prev = e - 1 if e != SHARED and passes[0] == 0 else -1
+            if prev >= 0 and not (final and True):
+                raw2 = load_second(prev, ("raw1_%d" % (n1 % RING)) if final else "raw2_%d" % prev)
+                n1 = n1 + (1 if final else 0)
+            if b == 1:
                 nc.sync.dma_start(out=gate_sb[:], in_=gate)
-            grouped1 = round_first(raw1, stage.tile([P, KP * PACK], BF16, name="grouped1", align_bytes=64), 2)
-            if s >= 1:
-                q3 = quantize(grouped3[s - 1], wq.tile([P, KP], U32, name="codes3", align_bytes=64))
-            if s >= 2:
-                hqs[s - 2] = quantize_hidden(hs[s - 2], s - 2, keep.tile([P, len(groups(s - 2)) * C], U32, name="h_codes%d" % s, align_bytes=64))
-            q1 = quantize(grouped1, wq.tile([P, KP], U32, name="codes1", align_bytes=64))
-            grouped3[s] = round_first(raw3, ring.tile([P, KP * PACK], BF16, name="grouped3_%d" % (s % HRING), align_bytes=64), 1 if s == last else 0)
-            if s >= 1:
-                hs[s - 1] = hidden(q3, acts[s - 1], s - 1)
-            acts[s] = activate(q1, s)
-            if due in raw2:
-                w2q[due] = quantize_second(raw2[due])
-            back = (s - 5) // 2 if s % 2 == 1 else -1
-            if back in w2q:
-                send_back(back)
-        for e in list(range(E - 2, E)) + [SHARED]:
-            raw2[e] = load_second(e)
-        q3 = quantize(grouped3[last], wq.tile([P, KP], U32, name="codes3", align_bytes=64))
-        hqs[last - 1] = quantize_hidden(hs[last - 1], last - 1, keep.tile([P, C], U32, name="h_codes_a", align_bytes=64))
-        hs[last] = hidden(q3, acts[last], last)
-        hqs[last] = quantize_hidden(hs[last], last, keep.tile([P, C], U32, name="h_codes_b", align_bytes=64))
-        for e in range(E - 2, E):
-            w2q[e] = quantize_second(raw2[e])
-            send_back(e)
-        w2q[SHARED] = quantize_second(raw2[SHARED])
+            q1s = []
+            for i, g in enumerate(passes):
+                grouped = round_first(raw1[:, :, i * KP:(i + 1) * KP], stage.tile([P, KP * PACK], BF16, name="grouped1", align_bytes=64), 1)
+                q1s.append(quantize(grouped, wq.tile([P, KP], U32, name="codes1", align_bytes=64)))
+            if False:
+                activate(q1s, ss, "acts_free")
+            grouped3 = [round_first(raw3s[i], stage.tile([P, KP * PACK], BF16, name="grouped3", align_bytes=64), 1) for i, g in enumerate(passes)]
+            if not (False):
+                activate(q1s, ss, name3 if True else "acts_%d" % (b % 2))
+            if prev >= 0:
+                w2q[prev] = quantize_second(raw2)
+                send_back(prev)
+            for i, s in enumerate(ss):
+                q3 = quantize(grouped3[i], wq.tile([P, KP], U32, name="codes3", align_bytes=64))
+                h = hidden(q3, acts[s], s)
+                hqs[s] = quantize_hidden(h, s, keep.tile([P, len(groups(s)) * C], U32, name="h_codes%d" % s, align_bytes=64))
+        raw2 = load_second(E - 1, "raw1_%d" % (n1 % RING))
+        raw2s = load_second(SHARED, "raw1_%d" % ((n1 + 1) % RING))
+        w2q[E - 1] = quantize_second(raw2)
+        send_back(E - 1)
+        w2q[SHARED] = quantize_second(raw2s)
         second_product(SHARED, ys_bank[:])
         for i in range(2):
             cols = slice(i * T // 2, (i + 1) * T // 2)

@@ -1,6 +1,7 @@
 from contextlib import ExitStack
 
 import concourse.mybir as mybir
+from concourse.masks import make_identity
 
 K, T, E, C, H, N = 512, 512, 4, 128, 1024, 128
 FLOPS = 2 * (E * C + T) * (2 * K * H + H * N)
@@ -22,7 +23,12 @@ KP = P * PACK
 PASSES = H // KP
 SHARED = E
 RING = 4
-HRING = 4
+CUT_W1 = [[-1,-1],[0,0],[-1,-1],[-1,-1],[-1,-1]]
+CUT_W3 = [[128,128],[-1,-1],[-1,-1],[-1,-1],[42,84]]
+CUT_W2 = {}
+SILU_HELD = [0,2,2,2,1]
+FIRST_LATE = 2
+LAST_CUT = 40
 
 
 def tile_moe_shr_glu_silu_kernel(tc, x_words, x_scales, w1, w3, w2, gate, offs, out):
@@ -30,10 +36,10 @@ def tile_moe_shr_glu_silu_kernel(tc, x_words, x_scales, w1, w3, w2, gate, offs, 
     with ExitStack() as ctx:
         keep = ctx.enter_context(tc.tile_pool(name="keep", bufs=1))
         ring = ctx.enter_context(tc.tile_pool(name="ring", bufs=1))
-        stage = ctx.enter_context(tc.tile_pool(name="stage", bufs=3))
-        wq = ctx.enter_context(tc.tile_pool(name="wq", bufs=4))
-        hp = ctx.enter_context(tc.tile_pool(name="hp", bufs=3))
-        pa = ctx.enter_context(tc.psum_pool(name="pa", bufs=4))
+        stage = ctx.enter_context(tc.tile_pool(name="stage", bufs=4))
+        wq = ctx.enter_context(tc.tile_pool(name="wq", bufs=6))
+        hp = ctx.enter_context(tc.tile_pool(name="hp", bufs=2))
+        pa = ctx.enter_context(tc.psum_pool(name="pa", bufs=3))
         pb = ctx.enter_context(tc.psum_pool(name="pb", bufs=2))
         py = ctx.enter_context(tc.psum_pool(name="py", bufs=1))
 
@@ -45,47 +51,59 @@ def tile_moe_shr_glu_silu_kernel(tc, x_words, x_scales, w1, w3, w2, gate, offs, 
         gate_sb = keep.tile([P, E * C], F32, name="gate_sb")
         routed = keep.tile([P, T], F32, name="routed")
         y_bank = py.tile([P, E * C], F32, name="y_bank")
-        ys_bank = py.tile([P, T], F32, name="ys_bank")
 
-        steps = [(e, g) for e in [SHARED] + list(range(E)) for g in range(PASSES)]
-        last = len(steps) - 1
-
-        def groups(s):
-            e = steps[s][0]
+        def groups(e):
             if e == SHARED:
                 return [(xw[:, i * C:(i + 1) * C], xs[:, i * C:(i + 1) * C]) for i in range(T // C)]
             return [(gw[:, e * C:(e + 1) * C], gs[:, e * C:(e + 1) * C])]
 
-        def load_first(w, e, passes, name):
-            raw = ring.tile([P, PACK, len(passes) * KP], F32, name=name)
-            nc.sync.dma_start(out=raw[:], in_=w[e].rearrange("(p j) c -> p j c", j=PACK)[:, :, passes[0] * KP:(passes[-1] + 1) * KP])
-            return raw
+        def load_first(w, e, g0, g1, name):
+            raw = ring.tile([P, PACK, (g1 - g0) * KP], F32, name=name)
+            nc.sync.dma_start(out=raw[:], in_=w[e].rearrange("(p j) c -> p j c", j=PACK)[:, :, g0 * KP:g1 * KP])
+            return [raw[:, :, i * KP:(i + 1) * KP] for i in range(g1 - g0)]
 
         def load_second(e, name):
             raw = ring.tile([P, PASSES, PACK * N], F32, name=name)
             nc.sync.dma_start(out=raw[:], in_=w2[e].rearrange("(g p j) n -> p g (j n)", p=P, j=PACK))
             return raw
 
-        def quantize(grouped, codes):
-            scales = wq.tile([P, codes.shape[1]], U8, name="scales", align_bytes=64, bufs=8)
-            nc.vector.quantize_mx(out=codes[:].bitcast(FP8X4), scales=scales[:], in_=grouped[:])
-            return codes, scales
-
-        def round_first(raw, grouped, cut):
+        def round_first(raw, cuts):
+            grouped = stage.tile([P, KP * PACK], BF16, name="grouped", align_bytes=64)
             dst = grouped[:].rearrange("p (u v m j) -> p u m j v", u=2, v=2, j=PACK)
             src = raw.rearrange("p j (m u v) -> p u m j v", u=2, v=2)
-            if cut > 0:
-                nc.vector.tensor_copy(out=dst[:, :cut], in_=src[:, :cut])
-            if cut < 2:
-                nc.scalar.copy(out=dst[:, cut:], in_=src[:, cut:])
+            cuts = (P, 0) if cuts == -1 else (cuts, cuts) if isinstance(cuts, int) else cuts
+            for u in range(2):
+                if cuts[u] > 0:
+                    nc.vector.tensor_copy(out=dst[:, u, :cuts[u]], in_=src[:, u, :cuts[u]])
+            if cuts[0] == cuts[1] and cuts[0] < P:
+                nc.scalar.copy(out=dst[:, :, cuts[0]:], in_=src[:, :, cuts[0]:])
+            elif cuts[0] != cuts[1]:
+                nc.scalar.copy(out=dst[:, 1, cuts[1]:], in_=src[:, 1, cuts[1]:])
             return grouped
 
-        def quantize_second(raw):
-            grouped = stage.tile([P, PASSES * N * PACK], BF16, name="grouped2", align_bytes=64)
+        def round_second(raw, on_vector):
+            grouped = stage.tile([P, PASSES * N * PACK], BF16, name="grouped2", align_bytes=64, bufs=2)
             dst = grouped[:].rearrange("p (g c i j) -> p g c j i", g=PASSES, i=4, j=PACK)
             src = raw[:].rearrange("p g (j c i) -> p g c j i", j=PACK, i=4)
-            nc.scalar.copy(out=dst, in_=src)
-            return quantize(grouped, wq.tile([P, PASSES * N], U32, name="codes2", align_bytes=64))
+            if on_vector < 0:
+                nc.scalar.copy(out=dst, in_=src)
+                return grouped
+            for g in range(PASSES):
+                if g < on_vector:
+                    nc.vector.tensor_copy(out=dst[:, g], in_=src[:, g])
+                else:
+                    nc.scalar.copy(out=dst[:, g], in_=src[:, g])
+            return grouped
+
+        def quantize(grouped, name, pool=wq, parts=1):
+            width = grouped.shape[1] // PACK
+            codes = pool.tile([P, width], U32, name=name + "_codes", align_bytes=64)
+            scales = pool.tile([P, width], U8, name=name + "_scales", align_bytes=64)
+            for i in range(parts):
+                cols = slice(i * width // parts, (i + 1) * width // parts)
+                nc.vector.quantize_mx(out=codes[:, cols].bitcast(FP8X4), scales=scales[:, cols],
+                                      in_=grouped[:, cols.start * PACK:cols.stop * PACK])
+            return codes, scales
 
         def first_product(wcs, tokens, bank):
             for t in range(PACK):
@@ -94,109 +112,112 @@ def tile_moe_shr_glu_silu_kernel(tc, x_words, x_scales, w1, w3, w2, gate, offs, 
                                     rhs=tokens[0].bitcast(FP8X4), rhs_scale=tokens[1], start=True, stop=True)
             return bank
 
-        def activate(q1s, ss, name):
-            act_all = ring.tile([P, sum(len(groups(s)) for s in ss), KP], F32, name=name)
-            i = 0
-            for q1, s in zip(q1s, ss):
-                acts[s] = []
-                for tokens in groups(s):
-                    a_bank = first_product(q1, tokens, pa.tile([P, PACK, C], F32, name="a_bank"))
-                    act = act_all[:, i, :].rearrange("p (c t d) -> p c t d", t=PACK, d=2)
-                    nc.scalar.activation(out=act, in_=a_bank[:].rearrange("p t (c d) -> p c t d", d=2), func=SILU, bias=zero[:])
-                    acts[s].append(act)
-                    i = i + 1
+        def activate(q1, e, room):
+            acts = []
+            for tokens in groups(e):
+                a_bank = first_product(q1, tokens, pa.tile([P, PACK, C], F32, name="a_bank"))
+                act = stage.tile([P, KP], F32, name="act", bufs=8)[:] if room is None else room
+                act = act.rearrange("p (c t d) -> p c t d", t=PACK, d=2)
+                nc.scalar.activation(out=act, in_=a_bank[:].rearrange("p t (c d) -> p c t d", d=2), func=SILU, bias=zero[:])
+                acts.append(act)
+            return acts
 
-        def hidden(q3, acts, s):
-            h = hp.tile([P, len(acts) * KP], BF16, name="h", align_bytes=64)
-            for i, tokens in enumerate(groups(s)):
+        def hidden(q3, acts, e, h):
+            for i, tokens in enumerate(groups(e)):
                 b_bank = first_product(q3, tokens, pb.tile([P, PACK, C], F32, name="b_bank"))
                 nc.vector.tensor_tensor(out=h[:, i * KP:(i + 1) * KP].rearrange("p (c d t) -> p c t d", d=2, t=PACK),
                                         in0=b_bank[:].rearrange("p t (c d) -> p c t d", d=2), in1=acts[i], op=MULT)
-            return h
 
-        def quantize_hidden(h, s, codes):
-            scales = keep.tile([P, codes.shape[1]], U8, name="h_scales%d" % s, align_bytes=64)
-            nc.vector.quantize_mx(out=codes[:].bitcast(FP8X4), scales=scales[:], in_=h[:])
-            return codes, scales
-
-        def second_product(e, bank):
-            q2 = w2q[e]
+        def second_product(q2, hqs, bank):
             for g in range(PASSES):
                 wc = slice(g * N, (g + 1) * N)
-                hq = hqs[steps.index((e, g))]
                 nc.tensor.matmul_mx(out=bank, lhsT=q2[0][:, wc].bitcast(FP8X4), lhsT_scale=q2[1][:, wc],
-                                    rhs=hq[0][:].bitcast(FP8X4), rhs_scale=hq[1][:], start=(g == 0), stop=(g == PASSES - 1))
+                                    rhs=hqs[g][0].bitcast(FP8X4), rhs_scale=hqs[g][1], start=(g == 0), stop=(g == PASSES - 1))
 
-        def send_back(e):
+        def send_back(e, q2, hqs, y_sb, bank):
             cols = slice(e * C, (e + 1) * C)
-            second_product(e, y_bank[:, cols])
-            y_sb = hp.tile([P, C], F32, name="y_sb")
-            nc.scalar.copy(out=y_sb[:], in_=y_bank[:, cols])
-            nc.vector.tensor_tensor(routed[:].indirect(offsets[:, e * C // 16:(e + 1) * C // 16]), y_sb[:], gate_sb[:, cols], MULT)
+            second_product(q2, hqs, bank)
+            nc.scalar.copy(out=y_sb, in_=bank)
+            nc.vector.tensor_tensor(routed[:].indirect(offsets[:, e * C // 16:(e + 1) * C // 16]), y_sb, gate_sb[:, cols], MULT)
 
         nc.vector.memset(xs[:].bitcast(I32), 0)
         zero_in = keep.tile([P, 1], F32, name="zero_in")
         zero = keep.tile([P, 1], F32, name="zero")
         nc.vector.memset(zero_in[:], 0.0)
         nc.scalar.activation(out=zero[:], in_=zero_in[:], func=SILU)
-        nc.sync.dma_start(offsets[:], offs)
         nc.sync.dma_start(out=xw[:], in_=x_words[0].rearrange("p t r -> p (t r)").bitcast(I32))
+        nc.sync.dma_start(offsets[:], offs)
+        gate_cols = keep.tile([P, PACK], F32, name="gate_cols")
+        nc.sync.dma_start(out=gate_cols[:], in_=gate[0].rearrange("(p j) -> p j", j=PACK))
         for r in range(4):
             nc.sync.dma_start(out=xs[:].bitcast(I32)[r:P:32, :], in_=x_scales[0].bitcast(I32)[r:16:4, :])
+        identity = keep.tile([P, P], F32, name="identity")
+        make_identity(nc, identity[:])
+        gate_bank = pa.tile([P, PACK, C], F32, name="a_bank")
+        for j in range(PACK):
+            nc.tensor.transpose(gate_bank[:, j, :], gate_cols[:, j:j + 1].to_broadcast([P, P]), identity[:])
+        nc.scalar.copy(out=gate_sb[:].rearrange("p (c j) -> p c j", j=PACK), in_=gate_bank[:].rearrange("p j c -> p c j"))
         half = E * C // 2
         for i in range(2):
             nc.vector.tensor_copy(gw[:, i * half:(i + 1) * half], xw[:].bitcast(U32).indirect(offsets[:, i * half // 16:(i + 1) * half // 16]))
-        for i in range(2):
-            nc.vector.tensor_copy(gs[:, i * half:(i + 1) * half], xs[:].indirect(offsets[:, i * half // 16:(i + 1) * half // 16]))
 
-        w2q, hqs, acts = {}, {}, {}
-        blocks = [(SHARED, [0, 1])] + [(e, [0, 1]) for e in range(E)]
-        n1 = 0
-        n3 = 0
-        for b, (e, passes) in enumerate(blocks):
-            final = b == len(blocks) - 1
-            ss = [steps.index((e, g)) for g in passes]
-            raw1 = load_first(w1, e, passes, "raw1_%d" % (n1 % RING))
-            n1 = n1 + 1
-            if final and True:
-                raw2 = load_second(e - 1, "raw1_%d" % (n1 % RING))
-                n1 = n1 + 1
-            raw3s = []
-            for part in ([[g] for g in passes] if final else [passes]):
-                name3 = "raw3_%d" % (n3 % RING)
-                raw = load_first(w3, e, part, name3)
-                raw3s.extend([raw[:, :, i * KP:(i + 1) * KP] for i in range(len(part))])
-                n3 = n3 + 1
-            prev = e - 1 if e != SHARED and passes[0] == 0 else -1
-            if prev >= 0 and not (final and True):
-                raw2 = load_second(prev, ("raw1_%d" % (n1 % RING)) if final else "raw2_%d" % prev)
-                n1 = n1 + (1 if final else 0)
-            if b == 1:
-                nc.sync.dma_start(out=gate_sb[:], in_=gate)
-            q1s = []
-            for i, g in enumerate(passes):
-                grouped = round_first(raw1[:, :, i * KP:(i + 1) * KP], stage.tile([P, KP * PACK], BF16, name="grouped1", align_bytes=64), 1)
-                q1s.append(quantize(grouped, wq.tile([P, KP], U32, name="codes1", align_bytes=64)))
-            if False:
-                activate(q1s, ss, "acts_free")
-            grouped3 = [round_first(raw3s[i], stage.tile([P, KP * PACK], BF16, name="grouped3", align_bytes=64), 1) for i, g in enumerate(passes)]
-            if not (False):
-                activate(q1s, ss, name3 if True else "acts_%d" % (b % 2))
-            if prev >= 0:
-                w2q[prev] = quantize_second(raw2)
-                send_back(prev)
-            for i, s in enumerate(ss):
-                q3 = quantize(grouped3[i], wq.tile([P, KP], U32, name="codes3", align_bytes=64))
-                h = hidden(q3, acts[s], s)
-                hqs[s] = quantize_hidden(h, s, keep.tile([P, len(groups(s)) * C], U32, name="h_codes%d" % s, align_bytes=64))
-        raw2 = load_second(E - 1, "raw1_%d" % (n1 % RING))
-        raw2s = load_second(SHARED, "raw1_%d" % ((n1 + 1) % RING))
-        w2q[E - 1] = quantize_second(raw2)
-        send_back(E - 1)
-        w2q[SHARED] = quantize_second(raw2s)
-        second_product(SHARED, ys_bank[:])
+        order = [SHARED] + list(range(E))
+        pending = None
+        hqs = {}
+        for b, e in enumerate(order):
+            final = b == len(order) - 1
+            raw1 = load_first(w1, e, 0, PASSES, "raw1_%d" % (b % RING))
+            if final:
+                raw3 = load_first(w3, e, 0, 1, "raw3_0") + load_first(w3, e, 1, 2, "raw3_1")
+            else:
+                raw3 = load_first(w3, e, 0, PASSES, "raw3_%d" % (b % RING))
+            if e < FIRST_LATE:
+                raw2 = load_second(e, "raw2_%d" % e)
+            grouped1 = [round_first(raw1[g], CUT_W1[b][g]) for g in range(PASSES)]
+            q1 = [quantize(grouped1[g][:], "w") for g in range(PASSES)]
+            if e == SHARED:
+                for i in range(2):
+                    nc.vector.tensor_copy(gs[:, i * half:(i + 1) * half], xs[:].indirect(offsets[:, i * half // 16:(i + 1) * half // 16]))
+            if pending is not None:
+                send_back(*pending, raw1[1][:, 0, KP - C:KP], y_bank[:, pending[0] * C:(pending[0] + 1) * C])
+                pending = None
+            held = SILU_HELD[b]
+            acts = [None, None]
+            for g in range(PASSES):
+                if held == 0 or (held > 2 and g == 0):
+                    acts[g] = activate(q1[g], e, None)
+            grouped3 = [round_first(raw3[g], (P, LAST_CUT) if final and g == 1 and LAST_CUT >= 0 else CUT_W3[b][g]) for g in range(PASSES)]
+            for g in range(PASSES):
+                if acts[g] is None:
+                    acts[g] = activate(q1[g], e, raw3[(held - 1) % 2][:, g, :])
+            q3 = [quantize(grouped3[g][:], "w", wq, 2 if final and g == 1 and LAST_CUT >= 0 else 1) for g in range(PASSES)]
+            width = len(groups(e)) * KP
+            if e == SHARED or final:
+                hqs[e] = []
+                for g in range(PASSES):
+                    h = hp.tile([P, width], BF16, name="h", align_bytes=64)
+                    hidden(q3[g], acts[g], e, h[:])
+                    hq = quantize(h[:], "h%d_%d" % (e, g), keep)
+                    hqs[e].append((hq[0][:], hq[1][:]))
+            else:
+                h = hp.tile([P, PASSES * width], BF16, name="h", align_bytes=64)
+                for g in range(PASSES):
+                    hidden(q3[g], acts[g], e, h[:, g * width:(g + 1) * width])
+                hq = quantize(h[:], "h%d" % e, keep)
+                hqs[e] = [(hq[0][:, g * C:(g + 1) * C], hq[1][:, g * C:(g + 1) * C]) for g in range(PASSES)]
+            if e < FIRST_LATE:
+                pending = (e, quantize(round_second(raw2, -1)[:], "w2", hp), hqs[e])
+        late = list(range(FIRST_LATE, E)) + [SHARED]
+        raw2s = [load_second(e, ["raw3_2", "raw1_3", "raw3_3"][i]) for i, e in enumerate(late)]
+        for e, raw2 in zip(late, raw2s):
+            q2 = quantize(round_second(raw2, CUT_W2.get(e, 0))[:], "w2", hp)
+            if e != SHARED:
+                y_sb = hp.tile([P, C], F32, name="y_sb")
+                send_back(e, q2, hqs[e], y_sb[:], pa.tile([P, PACK, C], F32, name="a_bank")[:, 0, :])
         for i in range(2):
             cols = slice(i * T // 2, (i + 1) * T // 2)
+            ys_bank = py.tile([P, T // 2], F32, name="ys_bank%d" % i)
+            second_product(q2, [(hq[0][:, cols], hq[1][:, cols]) for hq in hqs[SHARED]], ys_bank[:])
             res = hp.tile([P, T // 2], F32, name="res")
-            nc.vector.tensor_tensor(out=res[:], in0=ys_bank[:, cols], in1=routed[:, cols], op=ADD)
-            nc.sync.dma_start(out=out[:, cols], in_=res[:])
+            nc.vector.tensor_tensor(out=res[:], in0=ys_bank[:], in1=routed[:, cols], op=ADD)
+            (nc.sync, nc.scalar)[i].dma_start(out=out[:, cols], in_=res[:])

@@ -23,12 +23,6 @@ KP = P * PACK
 PASSES = H // KP
 SHARED = E
 RING = 4
-CUT_W1 = [[-1,-1],[0,0],[-1,-1],[-1,-1],[-1,-1]]
-CUT_W3 = [[128,128],[-1,-1],[-1,-1],[-1,-1],[42,84]]
-CUT_W2 = {}
-SILU_HELD = [0,2,2,2,1]
-FIRST_LATE = 2
-LAST_CUT = 40
 
 
 def tile_moe_shr_glu_silu_kernel(tc, x_words, x_scales, w1, w3, w2, gate, offs, out):
@@ -147,73 +141,188 @@ def tile_moe_shr_glu_silu_kernel(tc, x_words, x_scales, w1, w3, w2, gate, offs, 
         nc.scalar.activation(out=zero[:], in_=zero_in[:], func=SILU)
         nc.sync.dma_start(out=xw[:], in_=x_words[0].rearrange("p t r -> p (t r)").bitcast(I32))
         nc.sync.dma_start(offsets[:], offs)
-        gate_cols = keep.tile([P, PACK], F32, name="gate_cols")
-        nc.sync.dma_start(out=gate_cols[:], in_=gate[0].rearrange("(p j) -> p j", j=PACK))
         for r in range(4):
             nc.sync.dma_start(out=xs[:].bitcast(I32)[r:P:32, :], in_=x_scales[0].bitcast(I32)[r:16:4, :])
         identity = keep.tile([P, P], F32, name="identity")
         make_identity(nc, identity[:])
-        gate_bank = pa.tile([P, PACK, C], F32, name="a_bank")
-        for j in range(PACK):
-            nc.tensor.transpose(gate_bank[:, j, :], gate_cols[:, j:j + 1].to_broadcast([P, P]), identity[:])
-        nc.scalar.copy(out=gate_sb[:].rearrange("p (c j) -> p c j", j=PACK), in_=gate_bank[:].rearrange("p j c -> p c j"))
+        gate_rows = keep.tile([P, C], F32, name="gate_rows")
+        nc.gpsimd.memset(gate_rows[:], 0.0)
+        nc.sync.dma_start(out=gate_rows[0:E, :], in_=gate[0].rearrange("(e c) -> e c", e=E))
+        nc.tensor.transpose(y_bank[:, 0:C], gate_rows[:], identity[:])
+        gate_cols = keep.tile([P, E], F32, name="gate_cols")
+        nc.scalar.copy(out=gate_cols[:], in_=y_bank[:, 0:E])
+        for e in range(E):
+            nc.tensor.transpose(y_bank[:, e * C:(e + 1) * C], gate_cols[:, e:e + 1].to_broadcast([P, P]), identity[:])
+        nc.scalar.copy(out=gate_sb[:], in_=y_bank[:])
         half = E * C // 2
         for i in range(2):
             nc.vector.tensor_copy(gw[:, i * half:(i + 1) * half], xw[:].bitcast(U32).indirect(offsets[:, i * half // 16:(i + 1) * half // 16]))
 
-        order = [SHARED] + list(range(E))
-        pending = None
-        hqs = {}
-        for b, e in enumerate(order):
-            final = b == len(order) - 1
-            raw1 = load_first(w1, e, 0, PASSES, "raw1_%d" % (b % RING))
-            if final:
-                raw3 = load_first(w3, e, 0, 1, "raw3_0") + load_first(w3, e, 1, 2, "raw3_1")
-            else:
-                raw3 = load_first(w3, e, 0, PASSES, "raw3_%d" % (b % RING))
-            if e < FIRST_LATE:
-                raw2 = load_second(e, "raw2_%d" % e)
-            grouped1 = [round_first(raw1[g], CUT_W1[b][g]) for g in range(PASSES)]
-            q1 = [quantize(grouped1[g][:], "w") for g in range(PASSES)]
-            if e == SHARED:
-                for i in range(2):
-                    nc.vector.tensor_copy(gs[:, i * half:(i + 1) * half], xs[:].indirect(offsets[:, i * half // 16:(i + 1) * half // 16]))
-            if pending is not None:
-                send_back(*pending, raw1[1][:, 0, KP - C:KP], y_bank[:, pending[0] * C:(pending[0] + 1) * C])
-                pending = None
-            held = SILU_HELD[b]
-            acts = [None, None]
-            for g in range(PASSES):
-                if held == 0 or (held > 2 and g == 0):
-                    acts[g] = activate(q1[g], e, None)
-            grouped3 = [round_first(raw3[g], (P, LAST_CUT) if final and g == 1 and LAST_CUT >= 0 else CUT_W3[b][g]) for g in range(PASSES)]
-            for g in range(PASSES):
-                if acts[g] is None:
-                    acts[g] = activate(q1[g], e, raw3[(held - 1) % 2][:, g, :])
-            q3 = [quantize(grouped3[g][:], "w", wq, 2 if final and g == 1 and LAST_CUT >= 0 else 1) for g in range(PASSES)]
+        S = SHARED
+        raw, grp, q, acts, hs, hqs = {}, {}, {}, {}, {}, {}
+
+        def load(slot, *names):
+            size = lambda x: PACK * H if len(x) == 2 and x[0] != "C" else PACK * KP if x[0] != "C" else N * PACK * (PASSES if len(x) == 2 else 1)
+            room = ring.tile([P, sum(size(x) for x in names)], F32, name=slot)
+            at = 0
+            for x in names:
+                part = room[:, at:at + size(x)]
+                at = at + size(x)
+                e = int(x[1])
+                if x[0] == "C" and len(x) == 2:
+                    part = part.rearrange("p (g c) -> p g c", g=PASSES)
+                    nc.sync.dma_start(out=part, in_=w2[e].rearrange("(g p j) n -> p g (j n)", p=P, j=PACK))
+                    for g in range(PASSES):
+                        raw["C", e, g] = part[:, g, :]
+                    raw["C", e] = part
+                elif x[0] == "C":
+                    nc.sync.dma_start(out=part, in_=w2[e].rearrange("(g p j) n -> p g (j n)", p=P, j=PACK)[:, int(x[2]), :])
+                    raw["C", e, int(x[2])] = part
+                else:
+                    w = (w1 if x[0] == "A" else w3)[e].rearrange("(p j) c -> p j c", j=PACK)
+                    part = part.rearrange("p (j c) -> p j c", j=PACK)
+                    if len(x) == 2:
+                        nc.sync.dma_start(out=part, in_=w)
+                        for g in range(PASSES):
+                            raw[x[0], e, g] = part[:, :, g * KP:(g + 1) * KP]
+                    else:
+                        g = int(x[2])
+                        nc.sync.dma_start(out=part, in_=w[:, :, g * KP:(g + 1) * KP])
+                        raw[x[0], e, g] = part
+
+        def cast(m, e, g, cuts):
+            grp[m, e, g] = round_first(raw[m, e, g], cuts)
+
+        def quant(m, e, g, parts=1):
+            q[m, e, g] = quantize(grp[m, e, g][:], "w", wq, parts)
+
+        def silu(e, g, room=None):
+            acts[e, g] = activate(q["A", e, g], e, room)
+
+        def mult(e, g, joint=True):
             width = len(groups(e)) * KP
-            if e == SHARED or final:
-                hqs[e] = []
-                for g in range(PASSES):
-                    h = hp.tile([P, width], BF16, name="h", align_bytes=64)
-                    hidden(q3[g], acts[g], e, h[:])
-                    hq = quantize(h[:], "h%d_%d" % (e, g), keep)
-                    hqs[e].append((hq[0][:], hq[1][:]))
+            if joint:
+                if g == 0:
+                    hs[e] = hp.tile([P, PASSES * width], BF16, name="h", align_bytes=64)
+                hidden(q["B", e, g], acts[e, g], e, hs[e][:, g * width:(g + 1) * width])
             else:
-                h = hp.tile([P, PASSES * width], BF16, name="h", align_bytes=64)
+                hs[e, g] = hp.tile([P, width], BF16, name="h", align_bytes=64)
+                hidden(q["B", e, g], acts[e, g], e, hs[e, g][:])
+
+        def hquant(e, g=None):
+            if g is None:
+                hq = quantize(hs[e][:], "h%d" % e, keep)
+                hqs[e] = [(hq[0][:, i * C:(i + 1) * C], hq[1][:, i * C:(i + 1) * C]) for i in range(PASSES)]
+            else:
+                hq = quantize(hs[e, g][:], "h%d_%d" % (e, g), keep)
+                hqs.setdefault(e, []).append((hq[0][:], hq[1][:]))
+
+        def cast2(e, engines):
+            grouped = stage.tile([P, PASSES * N * PACK], BF16, name="grouped2", align_bytes=64, bufs=3)
+            dst = grouped[:].rearrange("p (g c i j) -> p g c j i", g=PASSES, i=4, j=PACK)
+            if engines == "S":
+                nc.scalar.copy(out=dst, in_=raw["C", e].rearrange("p g (j c i) -> p g c j i", j=PACK, i=4))
+            else:
                 for g in range(PASSES):
-                    hidden(q3[g], acts[g], e, h[:, g * width:(g + 1) * width])
-                hq = quantize(h[:], "h%d" % e, keep)
-                hqs[e] = [(hq[0][:, g * C:(g + 1) * C], hq[1][:, g * C:(g + 1) * C]) for g in range(PASSES)]
-            if e < FIRST_LATE:
-                pending = (e, quantize(round_second(raw2, -1)[:], "w2", hp), hqs[e])
-        late = list(range(FIRST_LATE, E)) + [SHARED]
-        raw2s = [load_second(e, ["raw3_2", "raw1_3", "raw3_3"][i]) for i, e in enumerate(late)]
-        for e, raw2 in zip(late, raw2s):
-            q2 = quantize(round_second(raw2, CUT_W2.get(e, 0))[:], "w2", hp)
-            if e != SHARED:
-                y_sb = hp.tile([P, C], F32, name="y_sb")
-                send_back(e, q2, hqs[e], y_sb[:], pa.tile([P, PACK, C], F32, name="a_bank")[:, 0, :])
+                    src = raw["C", e, g].rearrange("p (j c i) -> p c j i", j=PACK, i=4)
+                    cut = engines[g]
+                    if cut > 0:
+                        nc.vector.tensor_copy(out=dst[:, g, :cut], in_=src[:, :cut])
+                    if cut < N // 4:
+                        nc.scalar.copy(out=dst[:, g, cut:], in_=src[:, cut:])
+            grp["C", e] = grouped
+
+        def quant2(e, parts=1):
+            q["C", e] = quantize(grp["C", e][:], "w2", hp, parts)
+
+        def back(e, room=None):
+            if room is None:
+                send_back(e, q["C", e], hqs[e], hp.tile([P, C], F32, name="y_sb")[:], pa.tile([P, PACK, C], F32, name="a_bank")[:, 0, :])
+            else:
+                send_back(e, q["C", e], hqs[e], room, y_bank[:, e * C:(e + 1) * C])
+
+        ys = {}
+
+        def yout(e, eng="S"):
+            bank = pa.tile([P, PACK, C], F32, name="a_bank")[:, 0, :]
+            second_product(q["C", e], hqs[e], bank)
+            ys[e] = hp.tile([P, C], F32, name="y_sb")
+            if eng == "S":
+                nc.scalar.copy(out=ys[e][:], in_=bank)
+            else:
+                nc.vector.tensor_copy(out=ys[e][:], in_=bank)
+
+        def scatter(e):
+            nc.vector.tensor_tensor(routed[:].indirect(offsets[:, e * C // 16:(e + 1) * C // 16]), ys[e][:], gate_sb[:, e * C:(e + 1) * C], MULT)
+
+        def gather_scales():
+            for i in range(2):
+                nc.vector.tensor_copy(gs[:, i * half:(i + 1) * half], xs[:].indirect(offsets[:, i * half // 16:(i + 1) * half // 16]))
+
+        load("raw1_0", "A4")
+        load("raw3_0", "B4")
+        for g in range(2): cast("A", S, g, -1)
+        for g in range(2): quant("A", S, g)
+        gather_scales()
+        for g in range(2): silu(S, g)
+        for g in range(2): cast("B", S, g, 128)
+        for g in range(2): quant("B", S, g)
+        for g in range(2):
+            mult(S, g, False)
+            hquant(S, g)
+        for e in range(2):
+            load("raw1_%d" % (e + 1), "A%d" % e)
+            load("raw3_%d" % (e + 1), "B%d" % e)
+            load("raw2_%d" % e, "C%d" % e)
+            for g in range(2): cast("A", e, g, 0 if e == 0 else -1)
+            for g in range(2): quant("A", e, g)
+            if e > 0: back(e - 1, raw["A", e, 1][:, 0, KP - C:KP])
+            for g in range(2): cast("B", e, g, -1)
+            for g in range(2): silu(e, g, raw["B", e, 1][:, g, :])
+            for g in range(2): quant("B", e, g)
+            for g in range(2): mult(e, g)
+            hquant(e)
+            cast2(e, "S")
+            quant2(e)
+
+        load("raw1_3", "A2")
+        load("raw3_3", "B2")
+        load("raw1_0", "A3")
+        load("raw3_0", "B30", "B31")
+        load("raw1_1", "C2", "C3", "C4")
+        for g in range(2): cast("A", 2, g, -1)
+        for g in range(2): quant("A", 2, g)
+        back(1, raw["A", 2, 1][:, 0, KP - C:KP])
+
+        cast("B", 2, 0, -1)
+        cast("B", 2, 1, -1)
+        for g in range(2): silu(2, g, raw["B", 2, 1][:, g, :])
+        for g in range(2): quant("B", 2, g)
+        for g in range(2): mult(2, g)
+        hquant(2)
+        cast("A", 3, 0, -1)
+        cast("A", 3, 1, -1)
+        for g in [0,1]: quant("A", 3, g)
+        cast("B", 3, 0, 42)
+        silu(3, 0, raw["B", 3, 0][:, 0, :])
+        silu(3, 1, raw["B", 3, 0][:, 1, :])
+        cast("B", 3, 1, (128,64))
+        quant("B", 3, 0)
+        quant("B", 3, 1, 2)
+        cast2(2, (0,0))
+        quant2(2, 2)
+        for g in range(2):
+            mult(3, g, False)
+            hquant(3, g)
+        yout(2, "S")
+        cast2(3, (0,0))
+        quant2(3, 2)
+        yout(3, "S")
+        cast2(S, (0,0))
+        quant2(S, 2)
+        scatter(2)
+        scatter(3)
+        q2 = q["C", S]
         for i in range(2):
             cols = slice(i * T // 2, (i + 1) * T // 2)
             ys_bank = py.tile([P, T // 2], F32, name="ys_bank%d" % i)

@@ -329,4 +329,4 @@ def tile_moe_shr_glu_silu_kernel(tc, x_words, x_scales, w1, w3, w2, gate, offs, 
             second_product(q2, [(hq[0][:, cols], hq[1][:, cols]) for hq in hqs[SHARED]], ys_bank[:])
             res = hp.tile([P, T // 2], F32, name="res")
             nc.vector.tensor_tensor(out=res[:], in0=ys_bank[:], in1=routed[:, cols], op=ADD)
-            (nc.sync, nc.scalar)[i].dma_start(out=out[:, cols], in_=res[:])
+            nc.sync.dma_start(out=out[:, cols], in_=res[:])

@@ -141,19 +141,6 @@ def tile_moe_shr_glu_silu_kernel(tc, x_words, x_scales, w1, w3, w2, gate, offs, 
         nc.scalar.activation(out=zero[:], in_=zero_in[:], func=SILU)
         nc.sync.dma_start(out=xw[:], in_=x_words[0].rearrange("p t r -> p (t r)").bitcast(I32))
         nc.sync.dma_start(offsets[:], offs)
-        for r in range(4):
-            nc.sync.dma_start(out=xs[:].bitcast(I32)[r:P:32, :], in_=x_scales[0].bitcast(I32)[r:16:4, :])
-        identity = keep.tile([P, P], F32, name="identity")
-        make_identity(nc, identity[:])
-        gate_rows = keep.tile([P, C], F32, name="gate_rows")
-        nc.gpsimd.memset(gate_rows[:], 0.0)
-        nc.sync.dma_start(out=gate_rows[0:E, :], in_=gate[0].rearrange("(e c) -> e c", e=E))
-        nc.tensor.transpose(y_bank[:, 0:C], gate_rows[:], identity[:])
-        gate_cols = keep.tile([P, E], F32, name="gate_cols")
-        nc.scalar.copy(out=gate_cols[:], in_=y_bank[:, 0:E])
-        for e in range(E):
-            nc.tensor.transpose(y_bank[:, e * C:(e + 1) * C], gate_cols[:, e:e + 1].to_broadcast([P, P]), identity[:])
-        nc.scalar.copy(out=gate_sb[:], in_=y_bank[:])
         half = E * C // 2
         for i in range(2):
             nc.vector.tensor_copy(gw[:, i * half:(i + 1) * half], xw[:].bitcast(U32).indirect(offsets[:, i * half // 16:(i + 1) * half // 16]))
@@ -260,6 +247,13 @@ def tile_moe_shr_glu_silu_kernel(tc, x_words, x_scales, w1, w3, w2, gate, offs, 
                 nc.vector.tensor_copy(gs[:, i * half:(i + 1) * half], xs[:].indirect(offsets[:, i * half // 16:(i + 1) * half // 16]))
 
         load("raw1_0", "A4")
+        for r in range(4):
+            nc.sync.dma_start(out=xs[:].bitcast(I32)[r:P:32, :], in_=x_scales[0].bitcast(I32)[r:16:4, :])
+        identity = keep.tile([P, P], F32, name="identity")
+        make_identity(nc, identity[:])
+        gate_rows = keep.tile([P, C], F32, name="gate_rows")
+        nc.gpsimd.memset(gate_rows[:], 0.0)
+        nc.sync.dma_start(out=gate_rows[0:E, :], in_=gate[0].rearrange("(e c) -> e c", e=E))
         load("raw3_0", "B4")
         for g in range(2): cast("A", S, g, -1)
         for g in range(2): quant("A", S, g)
@@ -270,6 +264,12 @@ def tile_moe_shr_glu_silu_kernel(tc, x_words, x_scales, w1, w3, w2, gate, offs, 
         for g in range(2):
             mult(S, g, False)
             hquant(S, g)
+        nc.tensor.transpose(y_bank[:, 0:C], gate_rows[:], identity[:])
+        gate_cols = keep.tile([P, E], F32, name="gate_cols")
+        nc.scalar.copy(out=gate_cols[:], in_=y_bank[:, 0:E])
+        for e in range(E):
+            nc.tensor.transpose(y_bank[:, e * C:(e + 1) * C], gate_cols[:, e:e + 1].to_broadcast([P, P]), identity[:])
+        nc.scalar.copy(out=gate_sb[:], in_=y_bank[:])
         for e in range(2):
             load("raw1_%d" % (e + 1), "A%d" % e)
             load("raw3_%d" % (e + 1), "B%d" % e)

@@ -72,7 +72,9 @@ def tile_moe_shr_glu_silu_kernel(tc, x_words, x_scales, w1, w3, w2, gate, offs, 
             if cuts[0] == cuts[1] and cuts[0] < P:
                 nc.scalar.copy(out=dst[:, :, cuts[0]:], in_=src[:, :, cuts[0]:])
             elif cuts[0] != cuts[1]:
-                nc.scalar.copy(out=dst[:, 1, cuts[1]:], in_=src[:, 1, cuts[1]:])
+                for u in (1, 0):
+                    if cuts[u] < P:
+                        nc.scalar.copy(out=dst[:, u, cuts[u]:], in_=src[:, u, cuts[u]:])
             return grouped
 
         def round_second(raw, on_vector):
@@ -242,6 +244,26 @@ def tile_moe_shr_glu_silu_kernel(tc, x_words, x_scales, w1, w3, w2, gate, offs, 
         def scatter(e):
             nc.vector.tensor_tensor(routed[:].indirect(offsets[:, e * C // 16:(e + 1) * C // 16]), ys[e][:], gate_sb[:, e * C:(e + 1) * C], MULT)
 
+        def load_cut(slot, e, cut):
+            room = ring.tile([P, PACK, H], F32, name=slot)
+            w = w3[e].rearrange("(p j) c -> p j c", j=PACK)
+            nc.sync.dma_start(out=room[:, :, :cut], in_=w[:, :, :cut])
+            nc.sync.dma_start(out=room[:, :, cut:], in_=w[:, :, cut:])
+            for g in range(PASSES):
+                raw["B", e, g] = room[:, :, g * KP:(g + 1) * KP]
+
+        def cast_parts(m, e, g, parts):
+            grouped = stage.tile([P, KP * PACK], BF16, name="grouped", align_bytes=64)
+            dst = grouped[:].rearrange("p (u v m j) -> p u m j v", u=2, v=2, j=PACK)
+            src = raw[m, e, g].rearrange("p j (m u v) -> p u m j v", u=2, v=2)
+            for eng, u0, u1, m0, m1 in parts:
+                if eng == "V":
+                    for u in range(u0, u1):
+                        nc.vector.tensor_copy(out=dst[:, u, m0:m1], in_=src[:, u, m0:m1])
+                else:
+                    nc.scalar.copy(out=dst[:, u0:u1, m0:m1], in_=src[:, u0:u1, m0:m1])
+            grp[m, e, g] = grouped
+
         def gather_scales():
             for i in range(2):
                 nc.vector.tensor_copy(gs[:, i * half:(i + 1) * half], xs[:].indirect(offsets[:, i * half // 16:(i + 1) * half // 16]))
@@ -306,11 +328,11 @@ def tile_moe_shr_glu_silu_kernel(tc, x_words, x_scales, w1, w3, w2, gate, offs, 
         cast("B", 3, 0, 42)
         silu(3, 0, raw["B", 3, 0][:, 0, :])
         silu(3, 1, raw["B", 3, 0][:, 1, :])
-        cast("B", 3, 1, (128,64))
+        cast("B", 3, 1, (128,96))
         quant("B", 3, 0)
         quant("B", 3, 1, 2)
         cast2(2, (0,0))
-        quant2(2, 2)
+        quant2(2, 1)
         for g in range(2):
             mult(3, g, False)
             hquant(3, g)
@@ -318,7 +340,7 @@ def tile_moe_shr_glu_silu_kernel(tc, x_words, x_scales, w1, w3, w2, gate, offs, 
         cast2(3, (0,0))
         quant2(3, 2)
         yout(3, "S")
-        cast2(S, (0,0))
+        cast2(S, (0,20))
         quant2(S, 2)
         scatter(2)
         scatter(3)

@@ -22,7 +22,15 @@ PACK = 4
 KP = P * PACK
 PASSES = H // KP
 SHARED = E
-RING = 4
+LAST = E - 1
+FIRST_LATE = E - 2
+RUN = 4
+
+HALVES = (P, 0)
+ALL_VECTOR = (P, P)
+ALL_SCALAR = (0, 0)
+LAST_W3_SHARES = ((42, 42), (P, 96))
+SHARED_W2_RUNS_ON_VECTOR = 12
 
 
 def tile_moe_shr_glu_silu_kernel(tc, x_words, x_scales, w1, w3, w2, gate, offs, out):
@@ -38,60 +46,81 @@ def tile_moe_shr_glu_silu_kernel(tc, x_words, x_scales, w1, w3, w2, gate, offs, 
         py = ctx.enter_context(tc.psum_pool(name="py", bufs=1))
 
         offsets = keep.tile([P, E * C // 16], U16, name="offsets")
-        xw = keep.tile([P, T], I32, name="xw", align_bytes=64)
-        xs = keep.tile([P, T], U8, name="xs", align_bytes=64)
-        gw = keep.tile([P, E * C], U32, name="gw", align_bytes=64)
-        gs = keep.tile([P, E * C], U8, name="gs", align_bytes=64)
+        words = keep.tile([P, T], I32, name="words", align_bytes=64)
+        scale_bytes = keep.tile([P, T], U8, name="scale_bytes", align_bytes=64)
+        slot_words = keep.tile([P, E * C], U32, name="slot_words", align_bytes=64)
+        slot_bytes = keep.tile([P, E * C], U8, name="slot_bytes", align_bytes=64)
         gate_sb = keep.tile([P, E * C], F32, name="gate_sb")
         routed = keep.tile([P, T], F32, name="routed")
         y_bank = py.tile([P, E * C], F32, name="y_bank")
 
-        def groups(e):
+        def listed(first, count):
+            return offsets[:, first // 16:(first + count) // 16]
+
+        def token_groups(e):
             if e == SHARED:
-                return [(xw[:, i * C:(i + 1) * C], xs[:, i * C:(i + 1) * C]) for i in range(T // C)]
-            return [(gw[:, e * C:(e + 1) * C], gs[:, e * C:(e + 1) * C])]
+                return [(words[:, i * C:(i + 1) * C], scale_bytes[:, i * C:(i + 1) * C]) for i in range(T // C)]
+            return [(slot_words[:, e * C:(e + 1) * C], slot_bytes[:, e * C:(e + 1) * C])]
 
-        def load_first(w, e, g0, g1, name):
-            raw = ring.tile([P, PACK, (g1 - g0) * KP], F32, name=name)
-            nc.sync.dma_start(out=raw[:], in_=w[e].rearrange("(p j) c -> p j c", j=PACK)[:, :, g0 * KP:g1 * KP])
-            return [raw[:, :, i * KP:(i + 1) * KP] for i in range(g1 - g0)]
+        def gather(dst, window):
+            half = E * C // 2
+            for i in range(2):
+                nc.vector.tensor_copy(dst[:, i * half:(i + 1) * half], window.indirect(listed(i * half, half)))
 
-        def load_second(e, name):
-            raw = ring.tile([P, PASSES, PACK * N], F32, name=name)
-            nc.sync.dma_start(out=raw[:], in_=w2[e].rearrange("(g p j) n -> p g (j n)", p=P, j=PACK))
-            return raw
+        def load_first(w, e, slot):
+            raw = ring.tile([P, PACK * H], F32, name=slot)[:].rearrange("p (j c) -> p j c", j=PACK)
+            nc.sync.dma_start(out=raw, in_=w[e].rearrange("(p j) c -> p j c", j=PACK))
+            return [raw[:, :, g * KP:(g + 1) * KP] for g in range(PASSES)]
 
-        def round_first(raw, cuts):
+        def load_first_by_pass(w, e, slot):
+            room = ring.tile([P, PASSES * PACK * KP], F32, name=slot)
+            raws = []
+            for g in range(PASSES):
+                raw = room[:, g * PACK * KP:(g + 1) * PACK * KP].rearrange("p (j c) -> p j c", j=PACK)
+                nc.sync.dma_start(out=raw, in_=w[e].rearrange("(p j) c -> p j c", j=PACK)[:, :, g * KP:(g + 1) * KP])
+                raws.append(raw)
+            return raws
+
+        def load_second(experts, slot):
+            size = PASSES * PACK * N
+            room = ring.tile([P, len(experts) * size], F32, name=slot)
+            raws = {}
+            for i, e in enumerate(experts):
+                raws[e] = room[:, i * size:(i + 1) * size].rearrange("p (g c) -> p g c", g=PASSES)
+                nc.sync.dma_start(out=raws[e], in_=w2[e].rearrange("(g p j) n -> p g (j n)", p=P, j=PACK))
+            return raws
+
+        def round_first(raw, share):
             grouped = stage.tile([P, KP * PACK], BF16, name="grouped", align_bytes=64)
             dst = grouped[:].rearrange("p (u v m j) -> p u m j v", u=2, v=2, j=PACK)
             src = raw.rearrange("p j (m u v) -> p u m j v", u=2, v=2)
-            cuts = (P, 0) if cuts == -1 else (cuts, cuts) if isinstance(cuts, int) else cuts
             for u in range(2):
-                if cuts[u] > 0:
-                    nc.vector.tensor_copy(out=dst[:, u, :cuts[u]], in_=src[:, u, :cuts[u]])
-            if cuts[0] == cuts[1] and cuts[0] < P:
-                nc.scalar.copy(out=dst[:, :, cuts[0]:], in_=src[:, :, cuts[0]:])
-            elif cuts[0] != cuts[1]:
-                for u in (1, 0):
-                    if cuts[u] < P:
-                        nc.scalar.copy(out=dst[:, u, cuts[u]:], in_=src[:, u, cuts[u]:])
+                if share[u] > 0:
+                    nc.vector.tensor_copy(out=dst[:, u, :share[u]], in_=src[:, u, :share[u]])
+            if share[1] < P:
+                u0 = 0 if share[0] < P else 1
+                nc.scalar.copy(out=dst[:, u0:, share[1]:], in_=src[:, u0:, share[1]:])
             return grouped
 
-        def round_second(raw, on_vector):
-            grouped = stage.tile([P, PASSES * N * PACK], BF16, name="grouped2", align_bytes=64, bufs=2)
-            dst = grouped[:].rearrange("p (g c i j) -> p g c j i", g=PASSES, i=4, j=PACK)
-            src = raw[:].rearrange("p g (j c i) -> p g c j i", j=PACK, i=4)
-            if on_vector < 0:
-                nc.scalar.copy(out=dst, in_=src)
-                return grouped
-            for g in range(PASSES):
-                if g < on_vector:
-                    nc.vector.tensor_copy(out=dst[:, g], in_=src[:, g])
-                else:
-                    nc.scalar.copy(out=dst[:, g], in_=src[:, g])
+        def second_views(raw):
+            grouped = stage.tile([P, PASSES * N * PACK], BF16, name="grouped2", align_bytes=64, bufs=3)
+            dst = grouped[:].rearrange("p (g c i j) -> p g c j i", g=PASSES, i=RUN, j=PACK)
+            return grouped, dst, raw.rearrange("p g (j c i) -> p g c j i", j=PACK, i=RUN)
+
+        def round_second(raw):
+            grouped, dst, src = second_views(raw)
+            nc.scalar.copy(out=dst, in_=src)
             return grouped
 
-        def quantize(grouped, name, pool=wq, parts=1):
+        def round_second_by_pass(raw, runs_on_vector=0):
+            grouped, dst, src = second_views(raw)
+            nc.scalar.copy(out=dst[:, 0], in_=src[:, 0])
+            if runs_on_vector > 0:
+                nc.vector.tensor_copy(out=dst[:, 1, :runs_on_vector], in_=src[:, 1, :runs_on_vector])
+            nc.scalar.copy(out=dst[:, 1, runs_on_vector:], in_=src[:, 1, runs_on_vector:])
+            return grouped
+
+        def quantize(grouped, name, pool, parts=1):
             width = grouped.shape[1] // PACK
             codes = pool.tile([P, width], U32, name=name + "_codes", align_bytes=64)
             scales = pool.tile([P, width], U8, name=name + "_scales", align_bytes=64)
@@ -101,254 +130,142 @@ def tile_moe_shr_glu_silu_kernel(tc, x_words, x_scales, w1, w3, w2, gate, offs, 
                                       in_=grouped[:, cols.start * PACK:cols.stop * PACK])
             return codes, scales
 
-        def first_product(wcs, tokens, bank):
-            for t in range(PACK):
-                cols = slice(t * P, (t + 1) * P)
-                nc.tensor.matmul_mx(out=bank[:, t, :], lhsT=wcs[0][:, cols].bitcast(FP8X4), lhsT_scale=wcs[1][:, cols],
-                                    rhs=tokens[0].bitcast(FP8X4), rhs_scale=tokens[1], start=True, stop=True)
-            return bank
+        def product(bank, weights, cols, moving, start=True, stop=True):
+            nc.tensor.matmul_mx(out=bank, lhsT=weights[0][:, cols].bitcast(FP8X4), lhsT_scale=weights[1][:, cols],
+                                rhs=moving[0].bitcast(FP8X4), rhs_scale=moving[1], start=start, stop=stop)
 
-        def activate(q1, e, room):
+        def first_product(weights, tokens, bank):
+            for t in range(PACK):
+                product(bank[:, t, :], weights, slice(t * P, (t + 1) * P), tokens)
+            return bank[:].rearrange("p t (c d) -> p c t d", d=2)
+
+        def activate(q1, e, room=None):
             acts = []
-            for tokens in groups(e):
-                a_bank = first_product(q1, tokens, pa.tile([P, PACK, C], F32, name="a_bank"))
-                act = stage.tile([P, KP], F32, name="act", bufs=8)[:] if room is None else room
+            for tokens in token_groups(e):
+                sums = first_product(q1, tokens, pa.tile([P, PACK, C], F32, name="a_bank"))
+                act = stage.tile([P, KP], F32, name="act", bufs=PASSES * T // C)[:] if room is None else room
                 act = act.rearrange("p (c t d) -> p c t d", t=PACK, d=2)
-                nc.scalar.activation(out=act, in_=a_bank[:].rearrange("p t (c d) -> p c t d", d=2), func=SILU, bias=zero[:])
+                nc.scalar.activation(out=act, in_=sums, func=SILU, bias=zero[:])
                 acts.append(act)
             return acts
 
         def hidden(q3, acts, e, h):
-            for i, tokens in enumerate(groups(e)):
-                b_bank = first_product(q3, tokens, pb.tile([P, PACK, C], F32, name="b_bank"))
+            for i, tokens in enumerate(token_groups(e)):
+                sums = first_product(q3, tokens, pb.tile([P, PACK, C], F32, name="b_bank"))
                 nc.vector.tensor_tensor(out=h[:, i * KP:(i + 1) * KP].rearrange("p (c d t) -> p c t d", d=2, t=PACK),
-                                        in0=b_bank[:].rearrange("p t (c d) -> p c t d", d=2), in1=acts[i], op=MULT)
+                                        in0=sums, in1=acts[i], op=MULT)
 
-        def second_product(q2, hqs, bank):
+        def hidden_pass(q3, acts, e, g):
+            h = hp.tile([P, len(acts) * KP], BF16, name="h", align_bytes=64)
+            hidden(q3, acts, e, h[:])
+            codes, scales = quantize(h[:], "h%d_%d" % (e, g), keep)
+            return codes[:], scales[:]
+
+        def second_product(q2, hq, bank):
             for g in range(PASSES):
-                wc = slice(g * N, (g + 1) * N)
-                nc.tensor.matmul_mx(out=bank, lhsT=q2[0][:, wc].bitcast(FP8X4), lhsT_scale=q2[1][:, wc],
-                                    rhs=hqs[g][0].bitcast(FP8X4), rhs_scale=hqs[g][1], start=(g == 0), stop=(g == PASSES - 1))
+                product(bank, q2, slice(g * N, (g + 1) * N), hq[g], start=(g == 0), stop=(g == PASSES - 1))
 
-        def send_back(e, q2, hqs, y_sb, bank):
-            cols = slice(e * C, (e + 1) * C)
-            second_product(q2, hqs, bank)
-            nc.scalar.copy(out=y_sb, in_=bank)
-            nc.vector.tensor_tensor(routed[:].indirect(offsets[:, e * C // 16:(e + 1) * C // 16]), y_sb, gate_sb[:, cols], MULT)
+        def scatter(e, y):
+            nc.vector.tensor_tensor(routed[:].indirect(listed(e * C, C)), y, gate_sb[:, e * C:(e + 1) * C], MULT)
 
-        nc.vector.memset(xs[:].bitcast(I32), 0)
+        def late_result(q2, hq):
+            bank = pa.tile([P, PACK, C], F32, name="a_bank")[:, 0, :]
+            second_product(q2, hq, bank)
+            y = hp.tile([P, C], F32, name="y")
+            nc.scalar.copy(out=y[:], in_=bank)
+            return y[:]
+
+        def warm_up(weights):
+            product(y_bank[:], weights, slice(0, P), (words[:], scale_bytes[:]))
+
+        nc.vector.memset(scale_bytes[:].bitcast(I32), 0)
         zero_in = keep.tile([P, 1], F32, name="zero_in")
         zero = keep.tile([P, 1], F32, name="zero")
         nc.vector.memset(zero_in[:], 0.0)
         nc.scalar.activation(out=zero[:], in_=zero_in[:], func=SILU)
-        nc.sync.dma_start(out=xw[:], in_=x_words[0].rearrange("p t r -> p (t r)").bitcast(I32))
+        nc.sync.dma_start(out=words[:], in_=x_words[0].rearrange("p t r -> p (t r)").bitcast(I32))
         nc.sync.dma_start(offsets[:], offs)
-        half = E * C // 2
-        for i in range(2):
-            nc.vector.tensor_copy(gw[:, i * half:(i + 1) * half], xw[:].bitcast(U32).indirect(offsets[:, i * half // 16:(i + 1) * half // 16]))
+        gather(slot_words, words[:].bitcast(U32))
 
-        S = SHARED
-        raw, grp, q, acts, hs, hqs = {}, {}, {}, {}, {}, {}
-
-        def load(slot, *names):
-            size = lambda x: PACK * H if len(x) == 2 and x[0] != "C" else PACK * KP if x[0] != "C" else N * PACK * (PASSES if len(x) == 2 else 1)
-            room = ring.tile([P, sum(size(x) for x in names)], F32, name=slot)
-            at = 0
-            for x in names:
-                part = room[:, at:at + size(x)]
-                at = at + size(x)
-                e = int(x[1])
-                if x[0] == "C" and len(x) == 2:
-                    part = part.rearrange("p (g c) -> p g c", g=PASSES)
-                    nc.sync.dma_start(out=part, in_=w2[e].rearrange("(g p j) n -> p g (j n)", p=P, j=PACK))
-                    for g in range(PASSES):
-                        raw["C", e, g] = part[:, g, :]
-                    raw["C", e] = part
-                elif x[0] == "C":
-                    nc.sync.dma_start(out=part, in_=w2[e].rearrange("(g p j) n -> p g (j n)", p=P, j=PACK)[:, int(x[2]), :])
-                    raw["C", e, int(x[2])] = part
-                else:
-                    w = (w1 if x[0] == "A" else w3)[e].rearrange("(p j) c -> p j c", j=PACK)
-                    part = part.rearrange("p (j c) -> p j c", j=PACK)
-                    if len(x) == 2:
-                        nc.sync.dma_start(out=part, in_=w)
-                        for g in range(PASSES):
-                            raw[x[0], e, g] = part[:, :, g * KP:(g + 1) * KP]
-                    else:
-                        g = int(x[2])
-                        nc.sync.dma_start(out=part, in_=w[:, :, g * KP:(g + 1) * KP])
-                        raw[x[0], e, g] = part
-
-        def cast(m, e, g, cuts):
-            grp[m, e, g] = round_first(raw[m, e, g], cuts)
-
-        def quant(m, e, g, parts=1):
-            q[m, e, g] = quantize(grp[m, e, g][:], "w", wq, parts)
-
-        def silu(e, g, room=None):
-            acts[e, g] = activate(q["A", e, g], e, room)
-
-        def mult(e, g, joint=True):
-            width = len(groups(e)) * KP
-            if joint:
-                if g == 0:
-                    hs[e] = hp.tile([P, PASSES * width], BF16, name="h", align_bytes=64)
-                hidden(q["B", e, g], acts[e, g], e, hs[e][:, g * width:(g + 1) * width])
-            else:
-                hs[e, g] = hp.tile([P, width], BF16, name="h", align_bytes=64)
-                hidden(q["B", e, g], acts[e, g], e, hs[e, g][:])
-
-        def hquant(e, g=None):
-            if g is None:
-                hq = quantize(hs[e][:], "h%d" % e, keep)
-                hqs[e] = [(hq[0][:, i * C:(i + 1) * C], hq[1][:, i * C:(i + 1) * C]) for i in range(PASSES)]
-            else:
-                hq = quantize(hs[e, g][:], "h%d_%d" % (e, g), keep)
-                hqs.setdefault(e, []).append((hq[0][:], hq[1][:]))
-
-        def cast2(e, engines):
-            grouped = stage.tile([P, PASSES * N * PACK], BF16, name="grouped2", align_bytes=64, bufs=3)
-            dst = grouped[:].rearrange("p (g c i j) -> p g c j i", g=PASSES, i=4, j=PACK)
-            if engines == "S":
-                nc.scalar.copy(out=dst, in_=raw["C", e].rearrange("p g (j c i) -> p g c j i", j=PACK, i=4))
-            else:
-                for g in range(PASSES):
-                    src = raw["C", e, g].rearrange("p (j c i) -> p c j i", j=PACK, i=4)
-                    cut = engines[g]
-                    if cut > 0:
-                        nc.vector.tensor_copy(out=dst[:, g, :cut], in_=src[:, :cut])
-                    if cut < N // 4:
-                        nc.scalar.copy(out=dst[:, g, cut:], in_=src[:, cut:])
-            grp["C", e] = grouped
-
-        def quant2(e, parts=1):
-            q["C", e] = quantize(grp["C", e][:], "w2", hp, parts)
-
-        def back(e, room=None):
-            if room is None:
-                send_back(e, q["C", e], hqs[e], hp.tile([P, C], F32, name="y_sb")[:], pa.tile([P, PACK, C], F32, name="a_bank")[:, 0, :])
-            else:
-                send_back(e, q["C", e], hqs[e], room, y_bank[:, e * C:(e + 1) * C])
-
-        ys = {}
-
-        def yout(e, eng="S"):
-            bank = pa.tile([P, PACK, C], F32, name="a_bank")[:, 0, :]
-            second_product(q["C", e], hqs[e], bank)
-            ys[e] = hp.tile([P, C], F32, name="y_sb")
-            if eng == "S":
-                nc.scalar.copy(out=ys[e][:], in_=bank)
-            else:
-                nc.vector.tensor_copy(out=ys[e][:], in_=bank)
-
-        def scatter(e):
-            nc.vector.tensor_tensor(routed[:].indirect(offsets[:, e * C // 16:(e + 1) * C // 16]), ys[e][:], gate_sb[:, e * C:(e + 1) * C], MULT)
-
-        def load_cut(slot, e, cut):
-            room = ring.tile([P, PACK, H], F32, name=slot)
-            w = w3[e].rearrange("(p j) c -> p j c", j=PACK)
-            nc.sync.dma_start(out=room[:, :, :cut], in_=w[:, :, :cut])
-            nc.sync.dma_start(out=room[:, :, cut:], in_=w[:, :, cut:])
-            for g in range(PASSES):
-                raw["B", e, g] = room[:, :, g * KP:(g + 1) * KP]
-
-        def cast_parts(m, e, g, parts):
-            grouped = stage.tile([P, KP * PACK], BF16, name="grouped", align_bytes=64)
-            dst = grouped[:].rearrange("p (u v m j) -> p u m j v", u=2, v=2, j=PACK)
-            src = raw[m, e, g].rearrange("p j (m u v) -> p u m j v", u=2, v=2)
-            for eng, u0, u1, m0, m1 in parts:
-                if eng == "V":
-                    for u in range(u0, u1):
-                        nc.vector.tensor_copy(out=dst[:, u, m0:m1], in_=src[:, u, m0:m1])
-                else:
-                    nc.scalar.copy(out=dst[:, u0:u1, m0:m1], in_=src[:, u0:u1, m0:m1])
-            grp[m, e, g] = grouped
-
-        def gather_scales():
-            for i in range(2):
-                nc.vector.tensor_copy(gs[:, i * half:(i + 1) * half], xs[:].indirect(offsets[:, i * half // 16:(i + 1) * half // 16]))
-
-        load("raw1_0", "A4")
+        raw1 = load_first(w1, SHARED, "w1_slot0")
         for r in range(4):
-            nc.sync.dma_start(out=xs[:].bitcast(I32)[r:P:32, :], in_=x_scales[0].bitcast(I32)[r:16:4, :])
+            nc.sync.dma_start(out=scale_bytes[:].bitcast(I32)[r:P:32, :], in_=x_scales[0].bitcast(I32)[r:16:4, :])
         identity = keep.tile([P, P], F32, name="identity")
         make_identity(nc, identity[:])
         gate_rows = keep.tile([P, C], F32, name="gate_rows")
         nc.gpsimd.memset(gate_rows[:], 0.0)
         nc.sync.dma_start(out=gate_rows[0:E, :], in_=gate[0].rearrange("(e c) -> e c", e=E))
-        load("raw3_0", "B4")
-        for g in range(2): cast("A", S, g, -1)
-        for g in range(2): quant("A", S, g)
-        gather_scales()
-        for g in range(2): silu(S, g)
-        for g in range(2): cast("B", S, g, 128)
-        for g in range(2): quant("B", S, g)
-        for g in range(2):
-            mult(S, g, False)
-            hquant(S, g)
+        raw3 = load_first(w3, SHARED, "w3_slot0")
+
+        grouped1 = [round_first(raw, HALVES) for raw in raw1]
+        q1 = [quantize(grouped[:], "w", wq) for grouped in grouped1]
+        gather(slot_bytes, scale_bytes[:])
+        acts = [activate(q, SHARED) for q in q1]
+        grouped3 = [round_first(raw, ALL_VECTOR) for raw in raw3]
+        q3 = [quantize(grouped[:], "w", wq) for grouped in grouped3]
+        hq = {SHARED: [hidden_pass(q3[g], acts[g], SHARED, g) for g in range(PASSES)]}
+
         nc.tensor.transpose(y_bank[:, 0:C], gate_rows[:], identity[:])
         gate_cols = keep.tile([P, E], F32, name="gate_cols")
         nc.scalar.copy(out=gate_cols[:], in_=y_bank[:, 0:E])
         for e in range(E):
             nc.tensor.transpose(y_bank[:, e * C:(e + 1) * C], gate_cols[:, e:e + 1].to_broadcast([P, P]), identity[:])
         nc.scalar.copy(out=gate_sb[:], in_=y_bank[:])
-        for e in range(2):
-            load("raw1_%d" % (e + 1), "A%d" % e)
-            load("raw3_%d" % (e + 1), "B%d" % e)
-            load("raw2_%d" % e, "C%d" % e)
-            for g in range(2): cast("A", e, g, 0 if e == 0 else -1)
-            for g in range(2): quant("A", e, g)
-            if e > 0: back(e - 1, raw["A", e, 1][:, 0, KP - C:KP])
-            for g in range(2): cast("B", e, g, -1)
-            for g in range(2): silu(e, g, raw["B", e, 1][:, g, :])
-            for g in range(2): quant("B", e, g)
-            for g in range(2): mult(e, g)
-            hquant(e)
-            cast2(e, "S")
-            quant2(e)
 
-        load("raw1_3", "A2")
-        load("raw3_3", "B2")
-        load("raw1_0", "A3")
-        load("raw3_0", "B30", "B31")
-        load("raw1_1", "C2", "C3", "C4")
-        for g in range(2): cast("A", 2, g, -1)
-        for g in range(2): quant("A", 2, g)
-        back(1, raw["A", 2, 1][:, 0, KP - C:KP])
+        raw2, q2 = {}, {}
+        for e in range(LAST):
+            raw1 = load_first(w1, e, "w1_slot%d" % (e + 1))
+            raw3 = load_first(w3, e, "w3_slot%d" % (e + 1))
+            if e < FIRST_LATE:
+                raw2.update(load_second([e], "w2_slot%d" % e))
+            else:
+                last_raw1 = load_first(w1, LAST, "w1_slot0")
+                last_raw3 = load_first_by_pass(w3, LAST, "w3_slot0")
+                raw2.update(load_second([FIRST_LATE, LAST, SHARED], "w1_slot1"))
+            grouped1 = [round_first(raw, ALL_SCALAR if e == 0 else HALVES) for raw in raw1]
+            q1 = [quantize(grouped[:], "w", wq) for grouped in grouped1]
+            if e > 0:
+                bank = y_bank[:, (e - 1) * C:e * C]
+                y = raw1[1][:, 0, KP - C:KP]
+                second_product(q2[e - 1], hq[e - 1], bank)
+                nc.scalar.copy(out=y, in_=bank)
+                scatter(e - 1, y)
+            grouped3 = [round_first(raw, HALVES) for raw in raw3]
+            acts = [activate(q1[g], e, raw3[1][:, g, :]) for g in range(PASSES)]
+            q3 = [quantize(grouped[:], "w", wq) for grouped in grouped3]
+            h = hp.tile([P, PASSES * KP], BF16, name="h", align_bytes=64)
+            for g in range(PASSES):
+                hidden(q3[g], acts[g], e, h[:, g * KP:(g + 1) * KP])
+            codes, scales = quantize(h[:], "h%d" % e, keep)
+            hq[e] = [(codes[:, g * C:(g + 1) * C], scales[:, g * C:(g + 1) * C]) for g in range(PASSES)]
+            if e < FIRST_LATE:
+                q2[e] = quantize(round_second(raw2[e])[:], "w2", hp)
+        warm_up(q3[0])
 
-        cast("B", 2, 0, -1)
-        cast("B", 2, 1, -1)
-        for g in range(2): silu(2, g, raw["B", 2, 1][:, g, :])
-        for g in range(2): quant("B", 2, g)
-        for g in range(2): mult(2, g)
-        hquant(2)
-        cast("A", 3, 0, -1)
-        cast("A", 3, 1, -1)
-        for g in [0,1]: quant("A", 3, g)
-        cast("B", 3, 0, 42)
-        silu(3, 0, raw["B", 3, 0][:, 0, :])
-        silu(3, 1, raw["B", 3, 0][:, 1, :])
-        cast("B", 3, 1, (128,96))
-        quant("B", 3, 0)
-        quant("B", 3, 1, 2)
-        cast2(2, (0,0))
-        quant2(2, 1)
-        for g in range(2):
-            mult(3, g, False)
-            hquant(3, g)
-        yout(2, "S")
-        cast2(3, (0,0))
-        quant2(3, 2)
-        yout(3, "S")
-        cast2(S, (0,20))
-        quant2(S, 2)
-        scatter(2)
-        scatter(3)
-        q2 = q["C", S]
+        grouped1 = [round_first(raw, HALVES) for raw in last_raw1]
+        q1 = [quantize(grouped[:], "w", wq) for grouped in grouped1]
+        grouped3 = [round_first(last_raw3[0], LAST_W3_SHARES[0])]
+        acts = [activate(q1[g], LAST, last_raw3[0][:, g, :]) for g in range(PASSES)]
+        warm_up(q1[0])
+        grouped3.append(round_first(last_raw3[1], LAST_W3_SHARES[1]))
+        q3 = [quantize(grouped3[0][:], "w", wq), quantize(grouped3[1][:], "w", wq, parts=2)]
+        q2[FIRST_LATE] = quantize(round_second_by_pass(raw2[FIRST_LATE])[:], "w2", hp, parts=PASSES)
+        hq[LAST] = []
+        for g in range(PASSES):
+            hq[LAST].append(hidden_pass(q3[g], acts[g], LAST, g))
+            warm_up(q3[g])
+        ys = {FIRST_LATE: late_result(q2[FIRST_LATE], hq[FIRST_LATE])}
+        warm_up(q2[FIRST_LATE])
+        q2[LAST] = quantize(round_second_by_pass(raw2[LAST])[:], "w2", hp, parts=PASSES)
+        ys[LAST] = late_result(q2[LAST], hq[LAST])
+        q2[SHARED] = quantize(round_second_by_pass(raw2[SHARED], SHARED_W2_RUNS_ON_VECTOR)[:], "w2", hp, parts=PASSES)
+        for e in (FIRST_LATE, LAST):
+            scatter(e, ys[e])
+
         for i in range(2):
             cols = slice(i * T // 2, (i + 1) * T // 2)
-            ys_bank = py.tile([P, T // 2], F32, name="ys_bank%d" % i)
-            second_product(q2, [(hq[0][:, cols], hq[1][:, cols]) for hq in hqs[SHARED]], ys_bank[:])
-            res = hp.tile([P, T // 2], F32, name="res")
-            nc.vector.tensor_tensor(out=res[:], in0=ys_bank[:], in1=routed[:, cols], op=ADD)
-            nc.sync.dma_start(out=out[:, cols], in_=res[:])
+            bank = py.tile([P, T // 2], F32, name="shared_bank%d" % i)
+            second_product(q2[SHARED], [(codes[:, cols], scales[:, cols]) for codes, scales in hq[SHARED]], bank[:])
+            result = hp.tile([P, T // 2], F32, name="result")
+            nc.vector.tensor_tensor(out=result[:], in0=bank[:], in1=routed[:, cols], op=ADD)
+            nc.sync.dma_start(out=out[:, cols], in_=result[:])

@@ -24,13 +24,13 @@ PASSES = H // KP
 SHARED = E
 LAST = E - 1
 FIRST_LATE = E - 2
-RUN = 4
+RUN = 2
 
 HALVES = (P, 0)
 ALL_VECTOR = (P, P)
 ALL_SCALAR = (0, 0)
 LAST_W3_SHARES = ((42, 42), (P, 96))
-SHARED_W2_RUNS_ON_VECTOR = 12
+SHARED_W2_RUNS_ON_VECTOR = 24
 
 
 def tile_moe_shr_glu_silu_kernel(tc, x_words, x_scales, w1, w3, w2, gate, offs, out):
@@ -67,13 +67,13 @@ def tile_moe_shr_glu_silu_kernel(tc, x_words, x_scales, w1, w3, w2, gate, offs, 
             for i in range(2):
                 nc.vector.tensor_copy(dst[:, i * half:(i + 1) * half], window.indirect(listed(i * half, half)))
 
-        def load_first(w, e, slot):
-            raw = ring.tile([P, PACK * H], F32, name=slot)[:].rearrange("p (j c) -> p j c", j=PACK)
+        def load_first(w, e, buf):
+            raw = ring.tile([P, PACK * H], F32, name=buf)[:].rearrange("p (j c) -> p j c", j=PACK)
             nc.sync.dma_start(out=raw, in_=w[e].rearrange("(p j) c -> p j c", j=PACK))
             return [raw[:, :, g * KP:(g + 1) * KP] for g in range(PASSES)]
 
-        def load_first_by_pass(w, e, slot):
-            room = ring.tile([P, PASSES * PACK * KP], F32, name=slot)
+        def load_first_by_pass(w, e, buf):
+            room = ring.tile([P, PASSES * PACK * KP], F32, name=buf)
             raws = []
             for g in range(PASSES):
                 raw = room[:, g * PACK * KP:(g + 1) * PACK * KP].rearrange("p (j c) -> p j c", j=PACK)
@@ -81,9 +81,9 @@ def tile_moe_shr_glu_silu_kernel(tc, x_words, x_scales, w1, w3, w2, gate, offs, 
                 raws.append(raw)
             return raws
 
-        def load_second(experts, slot):
+        def load_second(experts, buf):
             size = PASSES * PACK * N
-            room = ring.tile([P, len(experts) * size], F32, name=slot)
+            room = ring.tile([P, len(experts) * size], F32, name=buf)
             raws = {}
             for i, e in enumerate(experts):
                 raws[e] = room[:, i * size:(i + 1) * size].rearrange("p (g c) -> p g c", g=PASSES)
@@ -187,7 +187,7 @@ def tile_moe_shr_glu_silu_kernel(tc, x_words, x_scales, w1, w3, w2, gate, offs, 
         nc.sync.dma_start(offsets[:], offs)
         gather(slot_words, words[:].bitcast(U32))
 
-        raw1 = load_first(w1, SHARED, "w1_slot0")
+        raw1 = load_first(w1, SHARED, "w1_buf0")
         for r in range(4):
             nc.sync.dma_start(out=scale_bytes[:].bitcast(I32)[r:P:32, :], in_=x_scales[0].bitcast(I32)[r:16:4, :])
         identity = keep.tile([P, P], F32, name="identity")
@@ -195,7 +195,7 @@ def tile_moe_shr_glu_silu_kernel(tc, x_words, x_scales, w1, w3, w2, gate, offs, 
         gate_rows = keep.tile([P, C], F32, name="gate_rows")
         nc.gpsimd.memset(gate_rows[:], 0.0)
         nc.sync.dma_start(out=gate_rows[0:E, :], in_=gate[0].rearrange("(e c) -> e c", e=E))
-        raw3 = load_first(w3, SHARED, "w3_slot0")
+        raw3 = load_first(w3, SHARED, "w3_buf0")
 
         grouped1 = [round_first(raw, HALVES) for raw in raw1]
         q1 = [quantize(grouped[:], "w", wq) for grouped in grouped1]
@@ -214,14 +214,14 @@ def tile_moe_shr_glu_silu_kernel(tc, x_words, x_scales, w1, w3, w2, gate, offs, 
 
         raw2, q2 = {}, {}
         for e in range(LAST):
-            raw1 = load_first(w1, e, "w1_slot%d" % (e + 1))
-            raw3 = load_first(w3, e, "w3_slot%d" % (e + 1))
+            raw1 = load_first(w1, e, "w1_buf%d" % (e + 1))
+            raw3 = load_first(w3, e, "w3_buf%d" % (e + 1))
             if e < FIRST_LATE:
-                raw2.update(load_second([e], "w2_slot%d" % e))
+                raw2.update(load_second([e], "w2_buf%d" % e))
             else:
-                last_raw1 = load_first(w1, LAST, "w1_slot0")
-                last_raw3 = load_first_by_pass(w3, LAST, "w3_slot0")
-                raw2.update(load_second([FIRST_LATE, LAST, SHARED], "w1_slot1"))
+                last_raw1 = load_first(w1, LAST, "w1_buf0")
+                last_raw3 = load_first_by_pass(w3, LAST, "w3_buf0")
+                raw2.update(load_second([FIRST_LATE, LAST, SHARED], "w1_buf1"))
             grouped1 = [round_first(raw, ALL_SCALAR if e == 0 else HALVES) for raw in raw1]
             q1 = [quantize(grouped[:], "w", wq) for grouped in grouped1]
             if e > 0:

@@ -30,7 +30,7 @@ HALVES = (P, 0)
 ALL_VECTOR = (P, P)
 ALL_SCALAR = (0, 0)
 LAST_W3_SHARES = ((42, 42), (P, 96))
-SHARED_W2_RUNS_ON_VECTOR = 24
+SHARED_W2_RUNS_ON_VECTOR = 64
 
 
 def tile_moe_shr_glu_silu_kernel(tc, x_words, x_scales, w1, w3, w2, gate, offs, out):
@@ -117,7 +117,8 @@ def tile_moe_shr_glu_silu_kernel(tc, x_words, x_scales, w1, w3, w2, gate, offs, 
             nc.scalar.copy(out=dst[:, 0], in_=src[:, 0])
             if runs_on_vector > 0:
                 nc.vector.tensor_copy(out=dst[:, 1, :runs_on_vector], in_=src[:, 1, :runs_on_vector])
-            nc.scalar.copy(out=dst[:, 1, runs_on_vector:], in_=src[:, 1, runs_on_vector:])
+            if runs_on_vector < N // RUN:
+                nc.scalar.copy(out=dst[:, 1, runs_on_vector:], in_=src[:, 1, runs_on_vector:])
             return grouped
 
         def quantize(grouped, name, pool, parts=1):

@@ -140,15 +140,19 @@ def tile_moe_shr_glu_silu_kernel(tc, x_words, x_scales, w1, w3, w2, gate, offs, 
                 product(bank[:, t, :], weights, slice(t * P, (t + 1) * P), tokens)
             return bank[:].rearrange("p t (c d) -> p c t d", d=2)
 
-        def activate(q1, e, room=None):
-            acts = []
-            for tokens in token_groups(e):
-                sums = first_product(q1, tokens, pa.tile([P, PACK, C], F32, name="a_bank"))
-                act = stage.tile([P, KP], F32, name="act", bufs=PASSES * T // C)[:] if room is None else room
-                act = act.rearrange("p (c t d) -> p c t d", t=PACK, d=2)
-                nc.scalar.activation(out=act, in_=sums, func=SILU, bias=zero[:])
-                acts.append(act)
-            return acts
+        def activate(q1, e, room):
+            sums = first_product(q1, token_groups(e)[0], pa.tile([P, PACK, C], F32, name="a_bank"))
+            act = room.rearrange("p (c t d) -> p c t d", t=PACK, d=2)
+            nc.scalar.activation(out=act, in_=sums, func=SILU, bias=zero[:])
+            return [act]
+
+        def activate_shared(q1):
+            act = stage.tile([P, PACK, T], F32, name="act", bufs=PASSES)
+            for t in range(PACK):
+                bank = pa.tile([P, PACK, C], F32, name="a_bank")[:].rearrange("p t c -> p (t c)")
+                product(bank, q1, slice(t * P, (t + 1) * P), (words[:], scale_bytes[:]))
+                nc.scalar.activation(out=act[:, t, :], in_=bank, func=SILU, bias=zero[:])
+            return [act[:, :, i * C:(i + 1) * C].rearrange("p t (c d) -> p c t d", d=2) for i in range(T // C)]
 
         def hidden(q3, acts, e, h):
             for i, tokens in enumerate(token_groups(e)):
@@ -176,9 +180,6 @@ def tile_moe_shr_glu_silu_kernel(tc, x_words, x_scales, w1, w3, w2, gate, offs, 
             nc.scalar.copy(out=y[:], in_=bank)
             return y[:]
 
-        def warm_up(weights):
-            product(y_bank[:], weights, slice(0, P), (words[:], scale_bytes[:]))
-
         nc.vector.memset(scale_bytes[:].bitcast(I32), 0)
         zero_in = keep.tile([P, 1], F32, name="zero_in")
         zero = keep.tile([P, 1], F32, name="zero")
@@ -201,7 +202,7 @@ def tile_moe_shr_glu_silu_kernel(tc, x_words, x_scales, w1, w3, w2, gate, offs, 
         grouped1 = [round_first(raw, HALVES) for raw in raw1]
         q1 = [quantize(grouped[:], "w", wq) for grouped in grouped1]
         gather(slot_bytes, scale_bytes[:])
-        acts = [activate(q, SHARED) for q in q1]
+        acts = [activate_shared(q) for q in q1]
         grouped3 = [round_first(raw, ALL_VECTOR) for raw in raw3]
         q3 = [quantize(grouped[:], "w", wq) for grouped in grouped3]
         hq = {SHARED: [hidden_pass(q3[g], acts[g], SHARED, g) for g in range(PASSES)]}
@@ -241,22 +242,18 @@ def tile_moe_shr_glu_silu_kernel(tc, x_words, x_scales, w1, w3, w2, gate, offs, 
             hq[e] = [(codes[:, g * C:(g + 1) * C], scales[:, g * C:(g + 1) * C]) for g in range(PASSES)]
             if e < FIRST_LATE:
                 q2[e] = quantize(round_second(raw2[e])[:], "w2", hp)
-        warm_up(q3[0])
 
         grouped1 = [round_first(raw, HALVES) for raw in last_raw1]
         q1 = [quantize(grouped[:], "w", wq) for grouped in grouped1]
         grouped3 = [round_first(last_raw3[0], LAST_W3_SHARES[0])]
         acts = [activate(q1[g], LAST, last_raw3[0][:, g, :]) for g in range(PASSES)]
-        warm_up(q1[0])
         grouped3.append(round_first(last_raw3[1], LAST_W3_SHARES[1]))
         q3 = [quantize(grouped3[0][:], "w", wq), quantize(grouped3[1][:], "w", wq, parts=2)]
         q2[FIRST_LATE] = quantize(round_second_by_pass(raw2[FIRST_LATE])[:], "w2", hp, parts=PASSES)
         hq[LAST] = []
         for g in range(PASSES):
             hq[LAST].append(hidden_pass(q3[g], acts[g], LAST, g))
-            warm_up(q3[g])
         ys = {FIRST_LATE: late_result(q2[FIRST_LATE], hq[FIRST_LATE])}
-        warm_up(q2[FIRST_LATE])
         q2[LAST] = quantize(round_second_by_pass(raw2[LAST])[:], "w2", hp, parts=PASSES)
         ys[LAST] = late_result(q2[LAST], hq[LAST])
         q2[SHARED] = quantize(round_second_by_pass(raw2[SHARED], SHARED_W2_RUNS_ON_VECTOR)[:], "w2", hp, parts=PASSES)

@@ -180,39 +180,47 @@ def tile_moe_shr_glu_silu_kernel(tc, x_words, x_scales, w1, w3, w2, gate, offs, 
             nc.scalar.copy(out=y[:], in_=bank)
             return y[:]
 
+        def warm_up(weights):
+            product(y_bank[:], weights, slice(0, P), (q3[0][0][:], q3[0][1][:]))
+
         nc.vector.memset(scale_bytes[:].bitcast(I32), 0)
+        nc.sync.dma_start(out=words[:], in_=x_words[0].rearrange("p t r -> p (t r)").bitcast(I32))
+        nc.sync.dma_start(offsets[:], offs)
+        scale_rows = keep.tile([P, T // 4], I32, name="scale_rows")
+        for q in range(4):
+            nc.scalar.dma_start(out=scale_rows[32 * q:32 * q + 4, :], in_=x_scales[0].bitcast(I32)[4 * q:4 * q + 4, :])
+        gate_in = keep.tile([E, C], F32, name="gate_in")
+        nc.scalar.dma_start(out=gate_in[:], in_=gate[0].rearrange("(e c) -> e c", e=E))
         zero_in = keep.tile([P, 1], F32, name="zero_in")
         zero = keep.tile([P, 1], F32, name="zero")
         nc.vector.memset(zero_in[:], 0.0)
         nc.scalar.activation(out=zero[:], in_=zero_in[:], func=SILU)
-        nc.sync.dma_start(out=words[:], in_=x_words[0].rearrange("p t r -> p (t r)").bitcast(I32))
-        nc.sync.dma_start(offsets[:], offs)
-        gather(slot_words, words[:].bitcast(U32))
-
         raw1 = load_first(w1, SHARED, "w1_buf0")
-        for r in range(4):
-            nc.sync.dma_start(out=scale_bytes[:].bitcast(I32)[r:P:32, :], in_=x_scales[0].bitcast(I32)[r:16:4, :])
+        raw3 = load_first(w3, SHARED, "w3_buf0")
+
+        gather(slot_words, words[:].bitcast(U32))
+        for q in range(4):
+            nc.vector.tensor_copy(out=scale_bytes[:].bitcast(I32)[32 * q:32 * q + 4, :], in_=scale_rows[32 * q:32 * q + 4, :])
+        gather(slot_bytes, scale_bytes[:])
+
         identity = keep.tile([P, P], F32, name="identity")
         make_identity(nc, identity[:])
         gate_rows = keep.tile([P, C], F32, name="gate_rows")
         nc.gpsimd.memset(gate_rows[:], 0.0)
-        nc.sync.dma_start(out=gate_rows[0:E, :], in_=gate[0].rearrange("(e c) -> e c", e=E))
-        raw3 = load_first(w3, SHARED, "w3_buf0")
-
-        grouped1 = [round_first(raw, HALVES) for raw in raw1]
-        q1 = [quantize(grouped[:], "w", wq) for grouped in grouped1]
-        gather(slot_bytes, scale_bytes[:])
-        acts = [activate_shared(q) for q in q1]
-        grouped3 = [round_first(raw, ALL_VECTOR) for raw in raw3]
-        q3 = [quantize(grouped[:], "w", wq) for grouped in grouped3]
-        hq = {SHARED: [hidden_pass(q3[g], acts[g], SHARED, g) for g in range(PASSES)]}
-
+        nc.scalar.copy(out=gate_rows[0:E, :], in_=gate_in[:])
         nc.tensor.transpose(y_bank[:, 0:C], gate_rows[:], identity[:])
         gate_cols = keep.tile([P, E], F32, name="gate_cols")
         nc.scalar.copy(out=gate_cols[:], in_=y_bank[:, 0:E])
         for e in range(E):
             nc.tensor.transpose(y_bank[:, e * C:(e + 1) * C], gate_cols[:, e:e + 1].to_broadcast([P, P]), identity[:])
         nc.scalar.copy(out=gate_sb[:], in_=y_bank[:])
+
+        grouped1 = [round_first(raw, HALVES) for raw in raw1]
+        q1 = [quantize(grouped[:], "w", wq) for grouped in grouped1]
+        acts = [activate_shared(q) for q in q1]
+        grouped3 = [round_first(raw, ALL_VECTOR) for raw in raw3]
+        q3 = [quantize(grouped[:], "w", wq) for grouped in grouped3]
+        hq = {SHARED: [hidden_pass(q3[g], acts[g], SHARED, g) for g in range(PASSES)]}
 
         raw2, q2 = {}, {}
         for e in range(LAST):
@@ -243,6 +251,7 @@ def tile_moe_shr_glu_silu_kernel(tc, x_words, x_scales, w1, w3, w2, gate, offs, 
             if e < FIRST_LATE:
                 q2[e] = quantize(round_second(raw2[e])[:], "w2", hp)
 
+
         grouped1 = [round_first(raw, HALVES) for raw in last_raw1]
         q1 = [quantize(grouped[:], "w", wq) for grouped in grouped1]
         grouped3 = [round_first(last_raw3[0], LAST_W3_SHARES[0])]
@@ -253,7 +262,9 @@ def tile_moe_shr_glu_silu_kernel(tc, x_words, x_scales, w1, w3, w2, gate, offs, 
         hq[LAST] = []
         for g in range(PASSES):
             hq[LAST].append(hidden_pass(q3[g], acts[g], LAST, g))
+            warm_up(q3[g])
         ys = {FIRST_LATE: late_result(q2[FIRST_LATE], hq[FIRST_LATE])}
+        warm_up(q2[FIRST_LATE])
         q2[LAST] = quantize(round_second_by_pass(raw2[LAST])[:], "w2", hp, parts=PASSES)
         ys[LAST] = late_result(q2[LAST], hq[LAST])
         q2[SHARED] = quantize(round_second_by_pass(raw2[SHARED], SHARED_W2_RUNS_ON_VECTOR)[:], "w2", hp, parts=PASSES)

@@ -24,13 +24,15 @@ PASSES = H // KP
 SHARED = E
 LAST = E - 1
 FIRST_LATE = E - 2
+BURST = 256
 RUN = 2
 
 HALVES = (P, 0)
 ALL_VECTOR = (P, P)
 ALL_SCALAR = (0, 0)
-LAST_W3_SHARES = ((42, 42), (P, 96))
-SHARED_W2_RUNS_ON_VECTOR = 64
+LAST_W1_SHARES = ((0, 0), (P, 16))
+LAST_W3_SHARES = ((80, 80), (P, 40))
+W3_BEFORE_LAST = (P, 32)
 
 
 def tile_moe_shr_glu_silu_kernel(tc, x_words, x_scales, w1, w3, w2, gate, offs, out):
@@ -40,13 +42,13 @@ def tile_moe_shr_glu_silu_kernel(tc, x_words, x_scales, w1, w3, w2, gate, offs, 
         ring = ctx.enter_context(tc.tile_pool(name="ring", bufs=1))
         stage = ctx.enter_context(tc.tile_pool(name="stage", bufs=4))
         wq = ctx.enter_context(tc.tile_pool(name="wq", bufs=6))
-        hp = ctx.enter_context(tc.tile_pool(name="hp", bufs=2))
+        hp = ctx.enter_context(tc.tile_pool(name="hp", bufs=3))
         pa = ctx.enter_context(tc.psum_pool(name="pa", bufs=3))
         pb = ctx.enter_context(tc.psum_pool(name="pb", bufs=2))
         py = ctx.enter_context(tc.psum_pool(name="py", bufs=1))
 
         offsets = keep.tile([P, E * C // 16], U16, name="offsets")
-        words = keep.tile([P, T], I32, name="words", align_bytes=64)
+        words = keep.tile([P, T], I32, name="words", align_bytes=BURST)
         scale_bytes = keep.tile([P, T], U8, name="scale_bytes", align_bytes=64)
         slot_words = keep.tile([P, E * C], U32, name="slot_words", align_bytes=64)
         slot_bytes = keep.tile([P, E * C], U8, name="slot_bytes", align_bytes=64)
@@ -68,37 +70,47 @@ def tile_moe_shr_glu_silu_kernel(tc, x_words, x_scales, w1, w3, w2, gate, offs, 
                 nc.vector.tensor_copy(dst[:, i * half:(i + 1) * half], window.indirect(listed(i * half, half)))
 
         def load_first(w, e, buf):
-            raw = ring.tile([P, PACK * H], F32, name=buf)[:].rearrange("p (j c) -> p j c", j=PACK)
+            raw = ring.tile([P, PACK * H], F32, name=buf, align_bytes=BURST)[:].rearrange("p (j c) -> p j c", j=PACK)
             nc.sync.dma_start(out=raw, in_=w[e].rearrange("(p j) c -> p j c", j=PACK))
             return [raw[:, :, g * KP:(g + 1) * KP] for g in range(PASSES)]
 
-        def load_first_by_pass(w, e, buf):
-            room = ring.tile([P, PASSES * PACK * KP], F32, name=buf)
+        def load_first_by_pass(w, e, buf, spare=0):
+            room = ring.tile([P, PASSES, PACK * KP + spare], F32, name=buf, align_bytes=BURST)
             raws = []
             for g in range(PASSES):
-                raw = room[:, g * PACK * KP:(g + 1) * PACK * KP].rearrange("p (j c) -> p j c", j=PACK)
+                raw = room[:, g, 0:PACK * KP].rearrange("p (j c) -> p j c", j=PACK)
                 nc.sync.dma_start(out=raw, in_=w[e].rearrange("(p j) c -> p j c", j=PACK)[:, :, g * KP:(g + 1) * KP])
                 raws.append(raw)
-            return raws
+            return raws, room
 
-        def load_second(experts, buf):
+        def load_second(experts, buf, by_pass=False):
             size = PASSES * PACK * N
-            room = ring.tile([P, len(experts) * size], F32, name=buf)
+            room = ring.tile([P, len(experts) * size], F32, name=buf, align_bytes=BURST)
             raws = {}
             for i, e in enumerate(experts):
                 raws[e] = room[:, i * size:(i + 1) * size].rearrange("p (g c) -> p g c", g=PASSES)
-                nc.sync.dma_start(out=raws[e], in_=w2[e].rearrange("(g p j) n -> p g (j n)", p=P, j=PACK))
+                source = w2[e].rearrange("(g p j) n -> p g (j n)", p=P, j=PACK)
+                if by_pass:
+                    for g in range(PASSES):
+                        nc.sync.dma_start(out=raws[e][:, g], in_=source[:, g])
+                else:
+                    nc.sync.dma_start(out=raws[e], in_=source)
             return raws
 
-        def round_first(raw, share):
-            grouped = stage.tile([P, KP * PACK], BF16, name="grouped", align_bytes=64)
-            dst = grouped[:].rearrange("p (u v m j) -> p u m j v", u=2, v=2, j=PACK)
+        def round_first(raw, share, grouped=None, first=0):
+            if grouped is None:
+                grouped = stage.tile([P, KP * PACK], BF16, name="grouped", align_bytes=64)
+            count = raw.shape[2] // PACK
+            dst = grouped[:].rearrange("p (u v m j) -> p u m j v", u=2, v=2, j=PACK)[:, :, first:first + count]
             src = raw.rearrange("p j (m u v) -> p u m j v", u=2, v=2)
-            for u in range(2):
-                if share[u] > 0:
-                    nc.vector.tensor_copy(out=dst[:, u, :share[u]], in_=src[:, u, :share[u]])
-            if share[1] < P:
-                u0 = 0 if share[0] < P else 1
+            if 0 < share[0] == share[1] < count:
+                nc.vector.tensor_copy(out=dst[:, :, :share[0]], in_=src[:, :, :share[0]])
+            else:
+                for u in range(2):
+                    if share[u] > 0:
+                        nc.vector.tensor_copy(out=dst[:, u, :share[u]], in_=src[:, u, :share[u]])
+            if share[1] < count:
+                u0 = 0 if share[0] < count else 1
                 nc.scalar.copy(out=dst[:, u0:, share[1]:], in_=src[:, u0:, share[1]:])
             return grouped
 
@@ -112,13 +124,10 @@ def tile_moe_shr_glu_silu_kernel(tc, x_words, x_scales, w1, w3, w2, gate, offs, 
             nc.scalar.copy(out=dst, in_=src)
             return grouped
 
-        def round_second_by_pass(raw, runs_on_vector=0):
+        def round_second_by_pass(raw):
             grouped, dst, src = second_views(raw)
-            nc.scalar.copy(out=dst[:, 0], in_=src[:, 0])
-            if runs_on_vector > 0:
-                nc.vector.tensor_copy(out=dst[:, 1, :runs_on_vector], in_=src[:, 1, :runs_on_vector])
-            if runs_on_vector < N // RUN:
-                nc.scalar.copy(out=dst[:, 1, runs_on_vector:], in_=src[:, 1, runs_on_vector:])
+            for g in range(PASSES):
+                nc.scalar.copy(out=dst[:, g], in_=src[:, g])
             return grouped
 
         def quantize(grouped, name, pool, parts=1):
@@ -142,7 +151,8 @@ def tile_moe_shr_glu_silu_kernel(tc, x_words, x_scales, w1, w3, w2, gate, offs, 
 
         def activate(q1, e, room):
             sums = first_product(q1, token_groups(e)[0], pa.tile([P, PACK, C], F32, name="a_bank"))
-            act = room.rearrange("p (c t d) -> p c t d", t=PACK, d=2)
+            act = room.rearrange("p r (c t d) -> p r c t d", t=PACK, d=2)
+            sums = sums.rearrange("p (r c) t d -> p r c t d", r=act.shape[1])
             nc.scalar.activation(out=act, in_=sums, func=SILU, bias=zero[:])
             return [act]
 
@@ -152,13 +162,13 @@ def tile_moe_shr_glu_silu_kernel(tc, x_words, x_scales, w1, w3, w2, gate, offs, 
                 bank = pa.tile([P, PACK, C], F32, name="a_bank")[:].rearrange("p t c -> p (t c)")
                 product(bank, q1, slice(t * P, (t + 1) * P), (words[:], scale_bytes[:]))
                 nc.scalar.activation(out=act[:, t, :], in_=bank, func=SILU, bias=zero[:])
-            return [act[:, :, i * C:(i + 1) * C].rearrange("p t (c d) -> p c t d", d=2) for i in range(T // C)]
+            return [act[:, :, i * C:(i + 1) * C].rearrange("p t (r c d) -> p r c t d", r=2, d=2) for i in range(T // C)]
 
         def hidden(q3, acts, e, h):
             for i, tokens in enumerate(token_groups(e)):
                 sums = first_product(q3, tokens, pb.tile([P, PACK, C], F32, name="b_bank"))
-                nc.vector.tensor_tensor(out=h[:, i * KP:(i + 1) * KP].rearrange("p (c d t) -> p c t d", d=2, t=PACK),
-                                        in0=sums, in1=acts[i], op=MULT)
+                nc.vector.tensor_tensor(out=h[:, i * KP:(i + 1) * KP].rearrange("p (r c d t) -> p r c t d", r=acts[i].shape[1], d=2, t=PACK),
+                                        in0=sums.rearrange("p (r c) t d -> p r c t d", r=acts[i].shape[1]), in1=acts[i], op=MULT)
 
         def hidden_pass(q3, acts, e, g):
             h = hp.tile([P, len(acts) * KP], BF16, name="h", align_bytes=64)
@@ -173,15 +183,14 @@ def tile_moe_shr_glu_silu_kernel(tc, x_words, x_scales, w1, w3, w2, gate, offs, 
         def scatter(e, y):
             nc.vector.tensor_tensor(routed[:].indirect(listed(e * C, C)), y, gate_sb[:, e * C:(e + 1) * C], MULT)
 
-        def late_result(q2, hq):
+        def late_result(q2, hq, y):
             bank = pa.tile([P, PACK, C], F32, name="a_bank")[:, 0, :]
             second_product(q2, hq, bank)
-            y = hp.tile([P, C], F32, name="y")
-            nc.scalar.copy(out=y[:], in_=bank)
-            return y[:]
+            nc.scalar.copy(out=y, in_=bank)
+            return y
 
-        def warm_up(weights):
-            product(y_bank[:], weights, slice(0, P), (q3[0][0][:], q3[0][1][:]))
+        def warm_up(weights, width=KP):
+            product(y_bank[:, 0:width], weights, slice(0, P), (q3[0][0][:, 0:width], q3[0][1][:, 0:width]))
 
         nc.vector.memset(scale_bytes[:].bitcast(I32), 0)
         nc.sync.dma_start(out=words[:], in_=x_words[0].rearrange("p t r -> p (t r)").bitcast(I32))
@@ -229,9 +238,9 @@ def tile_moe_shr_glu_silu_kernel(tc, x_words, x_scales, w1, w3, w2, gate, offs, 
             if e < FIRST_LATE:
                 raw2.update(load_second([e], "w2_buf%d" % e))
             else:
-                last_raw1 = load_first(w1, LAST, "w1_buf0")
-                last_raw3 = load_first_by_pass(w3, LAST, "w3_buf0")
-                raw2.update(load_second([FIRST_LATE, LAST, SHARED], "w1_buf1"))
+                last_raw1 = load_first_by_pass(w1, LAST, "w1_buf0")[0]
+                last_raw3, last_room = load_first_by_pass(w3, LAST, "w3_buf0", KP)
+                raw2.update(load_second([FIRST_LATE, LAST, SHARED], "w1_buf1", by_pass=True))
             grouped1 = [round_first(raw, ALL_SCALAR if e == 0 else HALVES) for raw in raw1]
             q1 = [quantize(grouped[:], "w", wq) for grouped in grouped1]
             if e > 0:
@@ -240,8 +249,8 @@ def tile_moe_shr_glu_silu_kernel(tc, x_words, x_scales, w1, w3, w2, gate, offs, 
                 second_product(q2[e - 1], hq[e - 1], bank)
                 nc.scalar.copy(out=y, in_=bank)
                 scatter(e - 1, y)
-            grouped3 = [round_first(raw, HALVES) for raw in raw3]
-            acts = [activate(q1[g], e, raw3[1][:, g, :]) for g in range(PASSES)]
+            grouped3 = [round_first(raw, W3_BEFORE_LAST if e == FIRST_LATE else HALVES) for raw in raw3]
+            acts = [activate(q1[g], e, raw3[1][:, g, :].rearrange("p (r c) -> p r c", r=2)) for g in range(PASSES)]
             q3 = [quantize(grouped[:], "w", wq) for grouped in grouped3]
             h = hp.tile([P, PASSES * KP], BF16, name="h", align_bytes=64)
             for g in range(PASSES):
@@ -252,29 +261,38 @@ def tile_moe_shr_glu_silu_kernel(tc, x_words, x_scales, w1, w3, w2, gate, offs, 
                 q2[e] = quantize(round_second(raw2[e])[:], "w2", hp)
 
 
-        grouped1 = [round_first(raw, HALVES) for raw in last_raw1]
+        grouped1 = [round_first(last_raw1[g], LAST_W1_SHARES[g]) for g in range(PASSES)]
         q1 = [quantize(grouped[:], "w", wq) for grouped in grouped1]
         grouped3 = [round_first(last_raw3[0], LAST_W3_SHARES[0])]
-        acts = [activate(q1[g], LAST, last_raw3[0][:, g, :]) for g in range(PASSES)]
+        tail = PACK * KP - C // 2
+        rooms = [last_raw3[0][:, :, KP - C - C // 2:KP - C // 2], last_room[:, 0, tail:tail + KP].rearrange("p (r c) -> p r c", r=PACK)]
+        acts = [activate(q1[g], LAST, rooms[g]) for g in range(PASSES)]
+        q3 = [quantize(grouped3[0][:], "w", wq)]
         grouped3.append(round_first(last_raw3[1], LAST_W3_SHARES[1]))
-        q3 = [quantize(grouped3[0][:], "w", wq), quantize(grouped3[1][:], "w", wq, parts=2)]
-        q2[FIRST_LATE] = quantize(round_second_by_pass(raw2[FIRST_LATE])[:], "w2", hp, parts=PASSES)
+        q3.append(quantize(grouped3[1][:], "w", wq, parts=2))
+        h = [last_raw3[1][:, 0, 0:KP // 2].bitcast(BF16), raw2[FIRST_LATE][:, 1, 0:KP // 2].bitcast(BF16)]
+        hidden(q3[0], acts[0], LAST, h[0])
+        warm_up(q3[0])
+        q2[FIRST_LATE] = quantize(round_second_by_pass(raw2[FIRST_LATE])[:], "w2", hp)
+        hidden(q3[1], acts[1], LAST, h[1])
+        warm_up(q3[1])
         hq[LAST] = []
         for g in range(PASSES):
-            hq[LAST].append(hidden_pass(q3[g], acts[g], LAST, g))
-            warm_up(q3[g])
-        ys = {FIRST_LATE: late_result(q2[FIRST_LATE], hq[FIRST_LATE])}
+            codes, scales = quantize(h[g], "h%d_%d" % (LAST, g), keep)
+            hq[LAST].append((codes[:], scales[:]))
+        q2[LAST] = quantize(round_second_by_pass(raw2[LAST])[:], "w2", hp)
+        ys = {FIRST_LATE: late_result(q2[FIRST_LATE], hq[FIRST_LATE], raw2[LAST][:, 0, 0:C])}
         warm_up(q2[FIRST_LATE])
-        q2[LAST] = quantize(round_second_by_pass(raw2[LAST])[:], "w2", hp, parts=PASSES)
-        ys[LAST] = late_result(q2[LAST], hq[LAST])
-        q2[SHARED] = quantize(round_second_by_pass(raw2[SHARED], SHARED_W2_RUNS_ON_VECTOR)[:], "w2", hp, parts=PASSES)
-        for e in (FIRST_LATE, LAST):
-            scatter(e, ys[e])
+        scatter(FIRST_LATE, ys[FIRST_LATE])
+        q2[SHARED] = quantize(round_second_by_pass(raw2[SHARED])[:], "w2", hp)
+        ys[LAST] = late_result(q2[LAST], hq[LAST], raw2[SHARED][:, 1, 0:C])
+        warm_up(q2[LAST], KP // 2)
+        scatter(LAST, ys[LAST])
 
         for i in range(2):
             cols = slice(i * T // 2, (i + 1) * T // 2)
             bank = py.tile([P, T // 2], F32, name="shared_bank%d" % i)
             second_product(q2[SHARED], [(codes[:, cols], scales[:, cols]) for codes, scales in hq[SHARED]], bank[:])
-            result = hp.tile([P, T // 2], F32, name="result")
+            result = hp.tile([P, T // 2], F32, name="result", align_bytes=BURST)
             nc.vector.tensor_tensor(out=result[:], in0=bank[:], in1=routed[:, cols], op=ADD)
             nc.sync.dma_start(out=out[:, cols], in_=result[:])

from contextlib import ExitStack

import concourse.mybir as mybir
from concourse.masks import make_identity

K, T, E, C, H, N = 512, 512, 4, 128, 1024, 128
FLOPS = 2 * (E * C + T) * (2 * K * H + H * N)

F32 = mybir.dt.float32
BF16 = mybir.dt.bfloat16
I32 = mybir.dt.int32
U32 = mybir.dt.uint32
U16 = mybir.dt.uint16
U8 = mybir.dt.uint8
FP8X4 = mybir.dt.float8_e4m3fn_x4
MULT = mybir.AluOpType.mult
ADD = mybir.AluOpType.add
SILU = mybir.ActivationFunctionType.Silu

P = 128
PACK = 4
KP = P * PACK
PASSES = H // KP
SHARED = E
LAST = E - 1
FIRST_LATE = E - 2
BURST = 256
RUN = 2

HALVES = (P, 0)
ALL_VECTOR = (P, P)
ALL_SCALAR = (0, 0)
LAST_W1_SHARES = ((0, 0), (P, 16))
LAST_W3_SHARES = ((80, 80), (P, 40))
W3_BEFORE_LAST = (P, 32)


def tile_moe_shr_glu_silu_kernel(tc, x_words, x_scales, w1, w3, w2, gate, offs, out):
    nc = tc.nc
    with ExitStack() as ctx:
        keep = ctx.enter_context(tc.tile_pool(name="keep", bufs=1))
        ring = ctx.enter_context(tc.tile_pool(name="ring", bufs=1))
        stage = ctx.enter_context(tc.tile_pool(name="stage", bufs=4))
        wq = ctx.enter_context(tc.tile_pool(name="wq", bufs=6))
        hp = ctx.enter_context(tc.tile_pool(name="hp", bufs=3))
        pa = ctx.enter_context(tc.psum_pool(name="pa", bufs=3))
        pb = ctx.enter_context(tc.psum_pool(name="pb", bufs=2))
        py = ctx.enter_context(tc.psum_pool(name="py", bufs=1))

        offsets = keep.tile([P, E * C // 16], U16, name="offsets")
        words = keep.tile([P, T], I32, name="words", align_bytes=BURST)
        scale_bytes = keep.tile([P, T], U8, name="scale_bytes", align_bytes=64)
        slot_words = keep.tile([P, E * C], U32, name="slot_words", align_bytes=64)
        slot_bytes = keep.tile([P, E * C], U8, name="slot_bytes", align_bytes=64)
        gate_sb = keep.tile([P, E * C], F32, name="gate_sb")
        routed = keep.tile([P, T], F32, name="routed")
        y_bank = py.tile([P, E * C], F32, name="y_bank")

        def listed(first, count):
            return offsets[:, first // 16:(first + count) // 16]

        def token_groups(e):
            if e == SHARED:
                return [(words[:, i * C:(i + 1) * C], scale_bytes[:, i * C:(i + 1) * C]) for i in range(T // C)]
            return [(slot_words[:, e * C:(e + 1) * C], slot_bytes[:, e * C:(e + 1) * C])]

        def gather(dst, window):
            half = E * C // 2
            for i in range(2):
                nc.vector.tensor_copy(dst[:, i * half:(i + 1) * half], window.indirect(listed(i * half, half)))

        def load_first(w, e, buf):
            raw = ring.tile([P, PACK * H], F32, name=buf, align_bytes=BURST)[:].rearrange("p (j c) -> p j c", j=PACK)
            nc.sync.dma_start(out=raw, in_=w[e].rearrange("(p j) c -> p j c", j=PACK))
            return [raw[:, :, g * KP:(g + 1) * KP] for g in range(PASSES)]

        def load_first_by_pass(w, e, buf, spare=0):
            room = ring.tile([P, PASSES, PACK * KP + spare], F32, name=buf, align_bytes=BURST)
            raws = []
            for g in range(PASSES):
                raw = room[:, g, 0:PACK * KP].rearrange("p (j c) -> p j c", j=PACK)
                nc.sync.dma_start(out=raw, in_=w[e].rearrange("(p j) c -> p j c", j=PACK)[:, :, g * KP:(g + 1) * KP])
                raws.append(raw)
            return raws, room

        def load_second(experts, buf, by_pass=False):
            size = PASSES * PACK * N
            room = ring.tile([P, len(experts) * size], F32, name=buf, align_bytes=BURST)
            raws = {}
            for i, e in enumerate(experts):
                raws[e] = room[:, i * size:(i + 1) * size].rearrange("p (g c) -> p g c", g=PASSES)
                source = w2[e].rearrange("(g p j) n -> p g (j n)", p=P, j=PACK)
                if by_pass:
                    for g in range(PASSES):
                        nc.sync.dma_start(out=raws[e][:, g], in_=source[:, g])
                else:
                    nc.sync.dma_start(out=raws[e], in_=source)
            return raws

        def round_first(raw, share, grouped=None, first=0):
            if grouped is None:
                grouped = stage.tile([P, KP * PACK], BF16, name="grouped", align_bytes=64)
            count = raw.shape[2] // PACK
            dst = grouped[:].rearrange("p (u v m j) -> p u m j v", u=2, v=2, j=PACK)[:, :, first:first + count]
            src = raw.rearrange("p j (m u v) -> p u m j v", u=2, v=2)
            if 0 < share[0] == share[1] < count:
                nc.vector.tensor_copy(out=dst[:, :, :share[0]], in_=src[:, :, :share[0]])
            else:
                for u in range(2):
                    if share[u] > 0:
                        nc.vector.tensor_copy(out=dst[:, u, :share[u]], in_=src[:, u, :share[u]])
            if share[1] < count:
                u0 = 0 if share[0] < count else 1
                nc.scalar.copy(out=dst[:, u0:, share[1]:], in_=src[:, u0:, share[1]:])
            return grouped

        def second_views(raw):
            grouped = stage.tile([P, PASSES * N * PACK], BF16, name="grouped2", align_bytes=64, bufs=3)
            dst = grouped[:].rearrange("p (g c i j) -> p g c j i", g=PASSES, i=RUN, j=PACK)
            return grouped, dst, raw.rearrange("p g (j c i) -> p g c j i", j=PACK, i=RUN)

        def round_second(raw):
            grouped, dst, src = second_views(raw)
            nc.scalar.copy(out=dst, in_=src)
            return grouped

        def round_second_by_pass(raw):
            grouped, dst, src = second_views(raw)
            for g in range(PASSES):
                nc.scalar.copy(out=dst[:, g], in_=src[:, g])
            return grouped

        def quantize(grouped, name, pool, parts=1):
            width = grouped.shape[1] // PACK
            codes = pool.tile([P, width], U32, name=name + "_codes", align_bytes=64)
            scales = pool.tile([P, width], U8, name=name + "_scales", align_bytes=64)
            for i in range(parts):
                cols = slice(i * width // parts, (i + 1) * width // parts)
                nc.vector.quantize_mx(out=codes[:, cols].bitcast(FP8X4), scales=scales[:, cols],
                                      in_=grouped[:, cols.start * PACK:cols.stop * PACK])
            return codes, scales

        def product(bank, weights, cols, moving, start=True, stop=True):
            nc.tensor.matmul_mx(out=bank, lhsT=weights[0][:, cols].bitcast(FP8X4), lhsT_scale=weights[1][:, cols],
                                rhs=moving[0].bitcast(FP8X4), rhs_scale=moving[1], start=start, stop=stop)

        def first_product(weights, tokens, bank):
            for t in range(PACK):
                product(bank[:, t, :], weights, slice(t * P, (t + 1) * P), tokens)
            return bank[:].rearrange("p t (c d) -> p c t d", d=2)

        def activate(q1, e, room):
            sums = first_product(q1, token_groups(e)[0], pa.tile([P, PACK, C], F32, name="a_bank"))
            act = room.rearrange("p r (c t d) -> p r c t d", t=PACK, d=2)
            sums = sums.rearrange("p (r c) t d -> p r c t d", r=act.shape[1])
            nc.scalar.activation(out=act, in_=sums, func=SILU, bias=zero[:])
            return [act]

        def activate_shared(q1):
            act = stage.tile([P, PACK, T], F32, name="act", bufs=PASSES)
            for t in range(PACK):
                bank = pa.tile([P, PACK, C], F32, name="a_bank")[:].rearrange("p t c -> p (t c)")
                product(bank, q1, slice(t * P, (t + 1) * P), (words[:], scale_bytes[:]))
                nc.scalar.activation(out=act[:, t, :], in_=bank, func=SILU, bias=zero[:])
            return [act[:, :, i * C:(i + 1) * C].rearrange("p t (r c d) -> p r c t d", r=2, d=2) for i in range(T // C)]

        def hidden(q3, acts, e, h):
            for i, tokens in enumerate(token_groups(e)):
                sums = first_product(q3, tokens, pb.tile([P, PACK, C], F32, name="b_bank"))
                nc.vector.tensor_tensor(out=h[:, i * KP:(i + 1) * KP].rearrange("p (r c d t) -> p r c t d", r=acts[i].shape[1], d=2, t=PACK),
                                        in0=sums.rearrange("p (r c) t d -> p r c t d", r=acts[i].shape[1]), in1=acts[i], op=MULT)

        def hidden_pass(q3, acts, e, g):
            h = hp.tile([P, len(acts) * KP], BF16, name="h", align_bytes=64)
            hidden(q3, acts, e, h[:])
            codes, scales = quantize(h[:], "h%d_%d" % (e, g), keep)
            return codes[:], scales[:]

        def second_product(q2, hq, bank):
            for g in range(PASSES):
                product(bank, q2, slice(g * N, (g + 1) * N), hq[g], start=(g == 0), stop=(g == PASSES - 1))

        def scatter(e, y):
            nc.vector.tensor_tensor(routed[:].indirect(listed(e * C, C)), y, gate_sb[:, e * C:(e + 1) * C], MULT)

        def late_result(q2, hq, y):
            bank = pa.tile([P, PACK, C], F32, name="a_bank")[:, 0, :]
            second_product(q2, hq, bank)
            nc.scalar.copy(out=y, in_=bank)
            return y

        def warm_up(weights, width=KP):
            product(y_bank[:, 0:width], weights, slice(0, P), (q3[0][0][:, 0:width], q3[0][1][:, 0:width]))

        nc.vector.memset(scale_bytes[:].bitcast(I32), 0)
        nc.sync.dma_start(out=words[:], in_=x_words[0].rearrange("p t r -> p (t r)").bitcast(I32))
        nc.sync.dma_start(offsets[:], offs)
        scale_rows = keep.tile([P, T // 4], I32, name="scale_rows")
        for q in range(4):
            nc.scalar.dma_start(out=scale_rows[32 * q:32 * q + 4, :], in_=x_scales[0].bitcast(I32)[4 * q:4 * q + 4, :])
        gate_in = keep.tile([E, C], F32, name="gate_in")
        nc.scalar.dma_start(out=gate_in[:], in_=gate[0].rearrange("(e c) -> e c", e=E))
        zero_in = keep.tile([P, 1], F32, name="zero_in")
        zero = keep.tile([P, 1], F32, name="zero")
        nc.vector.memset(zero_in[:], 0.0)
        nc.scalar.activation(out=zero[:], in_=zero_in[:], func=SILU)
        raw1 = load_first(w1, SHARED, "w1_buf0")
        raw3 = load_first(w3, SHARED, "w3_buf0")

        gather(slot_words, words[:].bitcast(U32))
        for q in range(4):
            nc.vector.tensor_copy(out=scale_bytes[:].bitcast(I32)[32 * q:32 * q + 4, :], in_=scale_rows[32 * q:32 * q + 4, :])
        gather(slot_bytes, scale_bytes[:])

        identity = keep.tile([P, P], F32, name="identity")
        make_identity(nc, identity[:])
        gate_rows = keep.tile([P, C], F32, name="gate_rows")
        nc.gpsimd.memset(gate_rows[:], 0.0)
        nc.scalar.copy(out=gate_rows[0:E, :], in_=gate_in[:])
        nc.tensor.transpose(y_bank[:, 0:C], gate_rows[:], identity[:])
        gate_cols = keep.tile([P, E], F32, name="gate_cols")
        nc.scalar.copy(out=gate_cols[:], in_=y_bank[:, 0:E])
        for e in range(E):
            nc.tensor.transpose(y_bank[:, e * C:(e + 1) * C], gate_cols[:, e:e + 1].to_broadcast([P, P]), identity[:])
        nc.scalar.copy(out=gate_sb[:], in_=y_bank[:])

        grouped1 = [round_first(raw, HALVES) for raw in raw1]
        q1 = [quantize(grouped[:], "w", wq) for grouped in grouped1]
        acts = [activate_shared(q) for q in q1]
        grouped3 = [round_first(raw, ALL_VECTOR) for raw in raw3]
        q3 = [quantize(grouped[:], "w", wq) for grouped in grouped3]
        hq = {SHARED: [hidden_pass(q3[g], acts[g], SHARED, g) for g in range(PASSES)]}

        raw2, q2 = {}, {}
        for e in range(LAST):
            raw1 = load_first(w1, e, "w1_buf%d" % (e + 1))
            raw3 = load_first(w3, e, "w3_buf%d" % (e + 1))
            if e < FIRST_LATE:
                raw2.update(load_second([e], "w2_buf%d" % e))
            else:
                last_raw1 = load_first_by_pass(w1, LAST, "w1_buf0")[0]
                last_raw3, last_room = load_first_by_pass(w3, LAST, "w3_buf0", KP)
                raw2.update(load_second([FIRST_LATE, LAST, SHARED], "w1_buf1", by_pass=True))
            grouped1 = [round_first(raw, ALL_SCALAR if e == 0 else HALVES) for raw in raw1]
            q1 = [quantize(grouped[:], "w", wq) for grouped in grouped1]
            if e > 0:
                bank = y_bank[:, (e - 1) * C:e * C]
                y = raw1[1][:, 0, KP - C:KP]
                second_product(q2[e - 1], hq[e - 1], bank)
                nc.scalar.copy(out=y, in_=bank)
                scatter(e - 1, y)
            grouped3 = [round_first(raw, W3_BEFORE_LAST if e == FIRST_LATE else HALVES) for raw in raw3]
            acts = [activate(q1[g], e, raw3[1][:, g, :].rearrange("p (r c) -> p r c", r=2)) for g in range(PASSES)]
            q3 = [quantize(grouped[:], "w", wq) for grouped in grouped3]
            h = hp.tile([P, PASSES * KP], BF16, name="h", align_bytes=64)
            for g in range(PASSES):
                hidden(q3[g], acts[g], e, h[:, g * KP:(g + 1) * KP])
            codes, scales = quantize(h[:], "h%d" % e, keep)
            hq[e] = [(codes[:, g * C:(g + 1) * C], scales[:, g * C:(g + 1) * C]) for g in range(PASSES)]
            if e < FIRST_LATE:
                q2[e] = quantize(round_second(raw2[e])[:], "w2", hp)


        grouped1 = [round_first(last_raw1[g], LAST_W1_SHARES[g]) for g in range(PASSES)]
        q1 = [quantize(grouped[:], "w", wq) for grouped in grouped1]
        grouped3 = [round_first(last_raw3[0], LAST_W3_SHARES[0])]
        tail = PACK * KP - C // 2
        rooms = [last_raw3[0][:, :, KP - C - C // 2:KP - C // 2], last_room[:, 0, tail:tail + KP].rearrange("p (r c) -> p r c", r=PACK)]
        acts = [activate(q1[g], LAST, rooms[g]) for g in range(PASSES)]
        q3 = [quantize(grouped3[0][:], "w", wq)]
        grouped3.append(round_first(last_raw3[1], LAST_W3_SHARES[1]))
        q3.append(quantize(grouped3[1][:], "w", wq, parts=2))
        h = [last_raw3[1][:, 0, 0:KP // 2].bitcast(BF16), raw2[FIRST_LATE][:, 1, 0:KP // 2].bitcast(BF16)]
        hidden(q3[0], acts[0], LAST, h[0])
        warm_up(q3[0])
        q2[FIRST_LATE] = quantize(round_second_by_pass(raw2[FIRST_LATE])[:], "w2", hp)
        hidden(q3[1], acts[1], LAST, h[1])
        warm_up(q3[1])
        hq[LAST] = []
        for g in range(PASSES):
            codes, scales = quantize(h[g], "h%d_%d" % (LAST, g), keep)
            hq[LAST].append((codes[:], scales[:]))
        q2[LAST] = quantize(round_second_by_pass(raw2[LAST])[:], "w2", hp)
        ys = {FIRST_LATE: late_result(q2[FIRST_LATE], hq[FIRST_LATE], raw2[LAST][:, 0, 0:C])}
        warm_up(q2[FIRST_LATE])
        scatter(FIRST_LATE, ys[FIRST_LATE])
        q2[SHARED] = quantize(round_second_by_pass(raw2[SHARED])[:], "w2", hp)
        ys[LAST] = late_result(q2[LAST], hq[LAST], raw2[SHARED][:, 1, 0:C])
        warm_up(q2[LAST], KP // 2)
        scatter(LAST, ys[LAST])

        for i in range(2):
            cols = slice(i * T // 2, (i + 1) * T // 2)
            bank = py.tile([P, T // 2], F32, name="shared_bank%d" % i)
            second_product(q2[SHARED], [(codes[:, cols], scales[:, cols]) for codes, scales in hq[SHARED]], bank[:])
            result = hp.tile([P, T // 2], F32, name="result", align_bytes=BURST)
            nc.vector.tensor_tensor(out=result[:], in0=bank[:], in1=routed[:, cols], op=ADD)
            nc.sync.dma_start(out=out[:, cols], in_=result[:])
